import numpy as np, ml_dtypes
CORES = [36,164,52,180,100,228,116,244]
N = 8
import mx_ref
BF = ml_dtypes.bfloat16
def gcols(t, e):
    v = np.concatenate([t.reshape(8, 16, -1, 4), np.zeros((8, 16, 1, 4), BF)], axis=2)
    return np.ascontiguousarray(np.stack([v[g][:, e[g]] for g in range(8)])).reshape(128, -1)
def tile(rs):
    return np.stack(rs, axis=2).reshape(128, -1).astype(BF)
def cut(t, i, w=512):
    return t[:, w * i:w * i + w]
def pick(q, e):
    c = np.concatenate([q[0].reshape(128, -1, 4), np.zeros((128, 1, 4), np.uint8)], axis=1); s = np.concatenate([q[1], np.ones((16, 1), np.uint8)], axis=1)
    return (np.ascontiguousarray(c[:, e].reshape(128, -1)), np.ascontiguousarray(s[:, e]))
def join(*qs):
    return (np.concatenate([q[0] for q in qs], axis=1), np.concatenate([q[1] for q in qs], axis=1))
def put(q, e, v):
    c, s = q[0].reshape(128, -1, 4).copy(), q[1].copy(); c[:, e] = v[0].reshape(128, -1, 4); s[:, e] = v[1]
    return (c.reshape(128, -1), s)
def pk(c, s):
    return (np.ascontiguousarray(c), mx_ref.live(s))
def emit(q):
    return q[0], q[1]
def packed(v, rng):
    q = [mx_ref.quantize(np.ascontiguousarray(v[r])) for r in range(N)]
    return np.stack([a for a, b in q]), np.stack([mx_ref.plane(b, rng) for a, b in q])
def values_of_codes():
    e, c = np.zeros((128, 128, 4), np.float32), np.zeros((128, 2, 4), np.uint8)
    e[np.arange(128), np.arange(128), 0] = 1
    c[:127, :, 0] = np.arange(256).reshape(2, 128).T[:127]
    return mx_ref.matmul(mx_ref.quantize(e.reshape(128, 512).astype(BF)), (c.reshape(128, 8), np.full((16, 2), 127, np.uint8))).T.reshape(-1).astype(np.float64)
CODE_VALUE, SCALE_VALUE = values_of_codes(), 2.0 ** (np.arange(256) - 127.0)
def decode(q):
    return (CODE_VALUE[q[0]].reshape(16, 8, -1, 4) * SCALE_VALUE[q[1]][:, None, :, None] + 0.0).reshape(128, -1).astype(np.float32)
def f(rng, *shape):
    return mx_ref.flush((rng.standard_normal(shape, dtype=np.float32) * np.exp2(rng.integers(-2, 3, shape[:-1] + (1,)))).astype(BF))
def wide(rng, *shape, cols=0):
    v = rng.standard_normal(shape, dtype=np.float32) * np.exp2(rng.integers(-12, 13, shape)).astype(np.float32)
    if cols: v *= np.repeat(np.exp2(rng.integers(-cols, cols + 1, shape[:-2] + (1, shape[-1] // 4))) * (rng.random(shape[:-2] + (1, shape[-1] // 4)) > 0.0625), 4, axis=-1).astype(np.float32)
    return mx_ref.flush(v.astype(BF))
C, A, R = 352, 128, 3
STEP = [1, 2, 4]
def parse(b, a):
    word = 64 * b[:, :-3] + 16 * b[:, 1:-2] + 4 * b[:, 2:-1] + b[:, 3:]
    block = 64 * a[:, ::4] + 16 * a[:, 1::4] + 4 * a[:, 2::4] + a[:, 3::4]
    first = np.full((8, 256), -1)
    for m in range(C // 4 - 1, -1, -1): first[np.arange(8), block[:, m]] = m
    found = np.concatenate([np.take_along_axis(first, word, axis=1), np.full((8, 3), -1)], axis=1)
    h = np.zeros((8, C), np.int64)
    go, shift, lits = np.zeros(8, np.int64), np.zeros(8, np.int64), np.zeros(8, np.int64)
    for c in range(C):
        run = (go == c) & (found[:, c] >= 0)
        lit = (go == c) & (found[:, c] < 0)
        shift = np.where(run, 4 * found[:, c] - c, shift)
        h[:, c] = np.where(lit, np.where(lits < A, C + c, c), c + shift)
        lits = lits + lit
        go = np.where(run, c + 4, np.where(lit, c + 1, go))
    return h
def numbers_of(rng):
    return {"x": np.array(f(rng, N, 128, 4 * C)), "u": np.array(f(rng, N, 128, 512)), "v": np.array(f(rng, N, 128, 512))}
def weights(rng, still=[]):
    w = np.array(f(rng, N, 128, 2048)).reshape(N, 8, 16, 4, 8, 16, 4)
    for i in still:
        w[:, :, i] = 0
        w[:, :, :, :, :, i] = 0
    c, p = packed(w.reshape(N, 128, 2048), rng)
    return {"wc": c, "ws": p}
def signs(rng):
    return np.stack([rng.permutation(8) % 2 * 2.0 - 1.0 for r in range(N)])
def planted(rng, z, size, k):
    d = numbers_of(rng)
    x = d["x"].astype(np.float32).reshape(N, 8, 16, C, 4)
    x[:, :, :8] = 0
    for i, b in enumerate((z // 2, z % 2)): x[:, :, i, :, 0] = np.where(b > 0, 1, -rng.integers(0, 2, z.shape)) * size
    u = d["u"].reshape(N, 128, 128, 4)
    for h in range(0, 128, 16):
        u[:, :, h:h + 2] = 0
        for i in range(2): u[:, h + i, h + i, 0] = k
    return {"x": x.reshape(N, 128, 4 * C).astype(BF), "u": u.reshape(N, 128, 512), "v": d["v"], **weights(rng, range(8))}
def setup_inputs(rng):
    return {**numbers_of(rng), **weights(rng)}
def setup_inputs_ties(rng):
    per = rng.permutation([1, 2, 3, 4, 5, 8, 12, 16])
    s = rng.integers(0, 240, (N, 8))
    z = np.zeros((N, 8, C), np.int64)
    for g in range(8):
        pat = rng.integers(0, 4, per[g])
        if per[g] == 1: pat[:] = rng.integers(1, 4)
        if per[g] == 4:
            pat = rng.permutation(4)
            s[1::2, g] = s[::2, g] + rng.integers(1, 4, N // 2)
        z[:, g] = pat[(s[:, g, None] + np.arange(C)) % per[g]]
        if per[g] in (1, 3):
            other = int(rng.choice(np.setdiff1d(np.arange(4), pat)))
            for r in range(0, N, 2): z[r, g, :int(rng.integers(1, 4))] = other
    d = planted(rng, z, 1.0, np.ones(N, np.float32).astype(BF))
    d["x"][rng.integers(N)] = 0
    return d
def setup_inputs_near(rng):
    low = rng.permutation(N) < N // 2
    size = np.exp2(np.where(low[:, None, None], -30.0, rng.integers(-30, 31, (N, 8, C))))
    d = planted(rng, rng.integers(0, 4, (N, 8, C)), size, np.where(low, 2.0 ** -30, 1.0).astype(np.float32).astype(BF))
    x, u = d["x"].reshape(N, 8, 16, C, 4), d["u"].reshape(N, 128, 128, 4)
    for r in range(N):
        if low[r]:
            k = x[r, :, :2, :, 0].astype(np.float32)
            least = (k > 0) & (rng.integers(0, 2, k.shape) > 0)
            x[r, :, :2, :, 0] = np.where(least, 2.25 * 2.0 ** -30, k).astype(np.float32).astype(BF)
            x[r, :, 2:4, :, 0] = np.where(least, -1.625 * 2.0 ** -30, 0.0).astype(np.float32).astype(BF)
            for h in range(0, 128, 16):
                for i in range(2): u[r, h + 2 + i, h + i, 0] = 1.375 * 2.0 ** -30
    return {"x": x.reshape(N, 128, 4 * C), "u": u.reshape(N, 128, 512), "v": d["v"], "wc": d["wc"], "ws": d["ws"]}
def setup_inputs_caps(rng):
    words = (rng.permutation(16)[:8, None] >> np.arange(4)) & 1
    late = rng.permutation(N // 2) % 2
    z = np.zeros((N, 8, C), np.int64)
    for r in range(N):
        if r % 2 == 0: h = int(rng.integers(8))
        n = np.insert(rng.permutation([0, 4, A - 4, A, A + 4, 2 * A, C - 32]), h, C)
        own = 2 + r % 2
        for g in range(8):
            if g == h:
                z[r, g] = own
                if late[r // 2]: z[r, g, r % 2 * (C - 4) + np.arange(4)] = words[0]
                continue
            k = rng.permutation(np.concatenate([np.full(n[g], -1), rng.integers(0, 8, (C - 32 - n[g]) // 4)]))
            mixed = np.concatenate([words[i] if i >= 0 else [own] for i in k])
            blocks = words[rng.permutation(8)].reshape(-1)
            z[r, g] = np.concatenate([mixed, blocks] if rng.integers(2) else [blocks, mixed])
    return planted(rng, z, 1.0, np.ones(N, np.float32).astype(BF))
def setup_inputs_huge(rng):
    d = numbers_of(rng)
    x = 2.0 ** 30 * (0.8 + 0.2 * rng.random((N, 128, C, 4)))
    for r in range(N): x[r][:, rng.permutation(C)[:C // 4 + 1]] = 2.0 ** 30
    c = np.ones((N, C))
    half = int(rng.integers(2))
    for r in range(N):
        if 2 * r // N == half: c[r] = rng.permutation(C) % 2 * 2.0 - 1.0
    x *= c[:, None, :, None]
    u = d["u"].reshape(N, 128, 8, 16, 4)
    h = int(rng.integers(8))
    s = np.stack([signs(rng), signs(rng)], axis=2)
    s = s * s[:, h:h + 1]
    a = 2.0 ** 30 * (1 - 0.1 * rng.random((N, 128, 8, 2, 4))) * s[:, None, :, :, None]
    a[:, :, h] = 2.0 ** 30
    u[:, :, :, :2] = a.astype(np.float32).astype(BF)
    w = np.zeros((N, 128, 4, 128, 4), np.float32)
    i = np.arange(128)
    for b in range(4): w[:, i, b, i, b] = -1
    wc, ws = packed(w.reshape(N, 128, 2048).astype(BF), rng)
    return {"x": x.astype(np.float32).reshape(N, 128, 4 * C).astype(BF), "u": u.reshape(N, 128, 512), "v": d["v"], "wc": wc, "ws": ws}
def setup_inputs_spread(rng):
    d = setup_inputs(rng)
    d["x"] = wide(rng, N, 128, 4 * C, cols=6)
    return d
def check_inputs(d):
    b = []
    for k in ("x", "u", "v"):
        a = np.abs(d[k].astype(np.float32))
        if not (np.isfinite(a).all() and ((a == 0) | (a >= 2.0 ** -30) & (a <= 2.0 ** 30)).all()): b.append("a value of " + k)
    if ((d["wc"] & 0x7F) == 0x7F).any(): b.append("a code of wc that is no number")
    z = np.zeros((128, 4, 4), np.float32)
    z[:, 1] = 2.0 ** -30
    z[:, 2] = 2.0 ** 30
    c, s = emit(mx_ref.quantize(z.reshape(128, 16).astype(BF)))
    for r in range(N):
        p = mx_ref.live(d["ws"][r])
        if not ((p == s[0, 0]) | (p >= s[0, 1]) & (p <= s[0, 2])).all(): b.append("a scale of ws")
    return b
def reference(x, u, v, wc, ws):
    qu = [mx_ref.quantize(u[r]) for r in range(N)]
    lay = [pk(wc[r], ws[r]) for r in range(N)]
    now = [x[r] for r in range(N)]
    for t in range(R):
        sent, z = [], []
        for r in range(N):
            q = mx_ref.quantize(now[r])
            p = mx_ref.matmul(qu[r], q)
            sent.append(q)
            z.append(2 * (p[::16] > 0).astype(np.int64) + (p[1::16] > 0))
        came = decode(join(*sent)).astype(BF)
        made, lists = [], []
        for r in range(N):
            e = r ^ STEP[t]
            h = parse(z[e], z[r])
            c = gcols(np.concatenate([now[r], cut(came, e, 4 * C)], axis=1), h)
            q = mx_ref.quantize(c)
            made.append(tile([mx_ref.matmul(pick(lay[r], np.arange(128 * b, 128 * b + 128)), q) * np.float32(0.015625) + c[:, b::4].astype(np.float32) for b in range(4)]))
            lists.append(h)
        now = made
    y, ot = np.zeros((N, 128, C), np.float32), np.zeros((N, 8, C), np.float32)
    oc, osc = np.zeros((N, 128, 4 * C), np.uint8), np.zeros((N, 16, C), np.uint8)
    for r in range(N):
        q = mx_ref.quantize(now[r])
        y[r] = mx_ref.matmul(mx_ref.quantize(v[r]), q)
        ot[r] = lists[r]
        oc[r], osc[r] = emit(q)
    return {"y": y, "ot": ot, "oc": oc, "osc": osc}

@@ -1,0 +1,322 @@
+from concourse.mybir import dt, AluOpType as A, ActivationFunctionType as F
+
+C = 352
+K = C // 16
+PL = 2 * C
+Q4, U8, BF, F32, I32, U16 = "float8_e4m3fn_x4", "uint8", "bfloat16", "float32", "int32", "uint16"
+
+
+def _sb(n, d):
+    return ("sbuf", [128, n], d)
+
+
+SCRATCH = {
+    "xin": _sb(4 * C, BF), "uin": _sb(512, BF), "vin": _sb(512, BF),
+    "qu": _sb(128, Q4), "su": _sb(128, U8), "qup": _sb(256, Q4), "sup": _sb(256, U8),
+    "qv": _sb(128, Q4), "sv": _sb(128, U8), "qw": _sb(512, Q4), "sw": _sb(512, U8),
+    "et": _sb(2048, BF), "qe": _sb(512, Q4), "se": _sb(512, U8),
+    "gt": _sb(4 * C, BF), "g64": _sb(4 * C, BF), "xt": _sb(4 * C, BF), "qg": _sb(C, Q4), "sg": _sb(C, U8),
+    "yb": _sb(C, F32),
+    "pcol": _sb(4, I32), "rint": _sb(4, I32), "rcol": _sb(4, F32), "bcol": _sb(4, F32), "j32": _sb(32, F32),
+    "t32": _sb(32, F32), "ca": _sb(32, F32), "cb": _sb(32, F32), "cc": _sb(32, F32), "cd": _sb(32, F32),
+    "ce": _sb(32, F32), "cf": _sb(16, F32), "cg": _sb(16, F32),
+    "ui": _sb(16, I32), "uoff": _sb(16, U16), "k16": _sb(24, F32), "pw": _sb(24, F32), "c352": _sb(24, F32),
+    "th0": _sb(8, F32), "th1": _sb(8, F32), "thm": _sb(8, F32), "dump": _sb(8, F32), "idn": _sb(128, F32),
+    "vals": _sb(96, F32), "alpha": _sb(C, BF), "mu32": _sb(C, BF), "mu4": _sb(C, BF), "m16": _sb(C, BF),
+    "mb": _sb(96, BF), "dbl": _sb(528, BF), "ones": _sb(C, BF), "inc": _sb(C, BF),
+    "za": _sb(C, BF), "zb": _sb(C, BF), "z": _sb(368, BF), "w2": _sb(PL, BF), "bs": _sb(384, BF),
+    "be": _sb(96, F32), "bw": _sb(8, F32), "eq": _sb(528, BF), "fs": _sb(528, BF), "dup": _sb(8, F32),
+    "dd": _sb(8, F32), "so": _sb(8, F32), "soff": _sb(8, U16), "gtab": _sb(272, BF),
+    "px": _sb(368, BF), "py": _sb(C, BF), "pd": _sb(C, BF), "keep": _sb(C, BF),
+    "d": _sb(368, BF), "q": _sb(C, BF), "pj": _sb(C, BF), "phi": _sb(C, BF), "pv": _sb(C, BF),
+    "v2": _sb(C, BF), "e1": _sb(C, BF), "e2": _sb(C, BF), "pa": _sb(C, BF), "rst": _sb(C, BF), "gm": _sb(368, BF),
+    "pz": _sb(C, BF), "nl": _sb(368, BF), "cnt": _sb(C, BF), "sgn": _sb(C, BF), "acc": _sb(4, F32),
+    "thr": _sb(4, F32), "st": _sb(C, BF), "d0": _sb(C, F32), "val": _sb(C, F32), "hh": _sb(C, F32),
+    "he": _sb(C, F32), "hi": _sb(24, I32), "hj": _sb(24, I32), "h1": _sb(24, F32), "hu": _sb(24, F32),
+    "hf": _sb(32, F32), "ht": _sb(32, F32), "off": _sb(24, U16),
+    "psa": ("psum", [128, 1024], F32), "psr": ("psum", [128, 2048], F32),
+}
+for _t in range(4):
+    SCRATCH["qx%d" % _t] = _sb(C, Q4)
+    SCRATCH["sx%d" % _t] = _sb(C, U8)
+for _t in range(3):
+    SCRATCH["lq%d" % _t] = _sb(C, Q4)
+    SCRATCH["ls%d" % _t] = _sb(C, U8)
+    SCRATCH["lw%d" % _t] = _sb(K, U16)
+    SCRATCH["ow%d" % _t] = _sb(K, U16)
+    SCRATCH["pl%d" % _t] = _sb(4 * PL, BF)
+    SCRATCH["tab%d" % _t] = _sb(360, F32)
+
+SEMAPHORES = (["V", "S", "T", "G", "ldx", "ldu", "ldw", "ldv", "stc", "sty", "sto", "sent",
+               "i0", "i1", "i2", "i3", "i4", "i5", "i6", "tb", "c0", "c1", "c2", "c3", "c4", "c5", "c6", "c7", "c8",
+               "qx", "sa", "sb", "w", "tab", "val", "pd", "phi", "pv", "v2", "cnt", "thr", "off", "gv", "gs", "qg",
+               "xs", "dcp", "qe", "qv", "ym", "yc", "ht", "pl"]
+              + ["%s%d" % (n, b) for n in ("r", "dm", "gb", "ya") for b in range(4)]
+              + ["%s%d" % (n, t) for n in ("as", "aw", "aq") for t in range(3)])
+
+EPS = 2.0 ** -13
+GRID = 2.0 ** 25
+
+
+def rank_program(g, core, T, topo):
+    rank = T.rank_of(core)
+    if rank is None:
+        return
+    queue = {"V": g.vector, "S": g.scalar, "T": g.tensor, "G": g, "Y": g.sync}
+    cnt, seen = {}, {e: {} for e in queue}
+
+    def wait(e, tok):
+        name, n = tok
+        if seen[e].get(name, 0) < n:
+            queue[e].wait_ge(T.sem[name], n)
+            seen[e][name] = n
+
+    def op(e, call, after=(), chain=True, sig=None, inc=1):
+        if chain and cnt.get(e, 0):
+            wait(e, (e, cnt[e]))
+        for tok in after:
+            wait(e, tok)
+        name = sig or e
+        call().then_inc(T.sem[name], inc)
+        cnt[name] = cnt.get(name, 0) + inc
+        return (name, cnt[name])
+
+    V, S = g.vector, g.scalar
+
+    def ts(out, in0, s1, o0, s2=None, o1=None, **k):
+        if o1 is None:
+            return op("V", lambda: V.tensor_scalar(out, in0, s1, None, o0), **k)
+        return op("V", lambda: V.tensor_scalar(out, in0, s1, s2, o0, o1), **k)
+
+    def tt(out, a, b, o, **k):
+        return op("V", lambda: V.tensor_tensor(out, a, b, o), **k)
+
+    def cp(out, a, **k):
+        return op("V", lambda: V.tensor_copy(out, a), **k)
+
+    def ms(out, c, **k):
+        return op("V", lambda: V.memset(out, c), **k)
+
+    def scan(out, a, b, init, o0, o1, **k):
+        return op("V", lambda: V.tensor_tensor_scan(out, a, b, init, o0, o1), **k)
+
+    def act(out, a, f, bias=0.0, scale=1.0, acc=None, **k):
+        if f == F.Copy and scale == 1.0:
+            return op("S", lambda: S.activation(out, a, f), **k)
+        if acc is not None:
+            return op("S", lambda: S.activation(out, a, f, bias=bias, scale=scale, accum_out=acc), **k)
+        return op("S", lambda: S.activation(out, a, f, bias=bias, scale=scale), **k)
+
+    def mm(out, lq, ls, rq, rs, **k):
+        return op("T", lambda: g.tensor.matmul_mx(out, lq, ls, rq, rs, True, True), chain=False, **k)
+
+    def quant(q, s, x, **k):
+        return op("V", lambda: V.quantize_mx(q, s, x), **k)
+
+    def iota(out, pat, base, cm, sig, fl=True):
+        if fl:
+            return op("G", lambda: g.iota(out, pat, base, cm, allow_small_or_imprecise_dtypes=True), chain=False, sig=sig)
+        return op("G", lambda: g.iota(out, pat, base, cm), chain=False, sig=sig)
+
+    def dma(e, out, a, sig, after=()):
+        return op(e, lambda: queue[e].dma_start(out, a), after=after, chain=False, sig=sig, inc=16)
+
+    def send(dst, out, a, sem, after):
+        for tok in after:
+            wait("G", tok)
+        rid, pid = topo.addr(dst, core)
+        n = len(topo.engines(core, dst))
+        g.remote_dma(out, a, T.sem[sem], T.sem["sent"], pid, rid, topo.mask(core, dst))
+        cnt["sent"] = cnt.get("sent", 0) + n
+        cnt[sem] = len(topo.engines(dst, core))
+        return (sem, cnt[sem])
+
+    def u8(v):
+        return v.bitcast(dt.uint8)
+
+    ldu = dma("S", T.uin[:], T.u[:], "ldu")
+    ldx = dma("Y", T.xin[:], T.x[:], "ldx")
+    dma("Y", u8(T.qw[:]), T.wc[:], "ldw")
+    ldw = dma("Y", T.sw[:], T.ws[:], "ldw")
+    ldv = dma("Y", T.vin[:], T.v[:], "ldv")
+
+    i0 = iota(T.pcol[:, 0:1], [[0, 1]], 0, 1, "i0", False)
+    i1 = iota(T.j32[:], [[1, 32]], 0, 0, "i1")
+    i2 = iota(T.ui[:], [[1, 2], [16, 8]], 0, 0, "i2", False)
+    i3 = iota(T.k16[:, 0:K], [[16, K]], 0, 0, "i3")
+    i4 = iota(T.vals[:], [[4, 96]], 0, 0, "i4")
+    i5 = iota(T.idn[:], [[-1, 128]], 0, 1, "i5")
+    i6 = iota(T.alpha[:], [[0, C // 4], [-1, 4]], 7, 0, "i6")
+
+    ms(T.mu4[:], 4.0)
+    ms(T.z[:, C:368], 0.0, chain=False)
+    ms(T.bs[:, C:384], 0.0, chain=False)
+    ms(T.dbl[:], 1.0, chain=False)
+    ts(T.rint[:, 0:1], T.pcol[:, 0:1], 15, A.bitwise_and, after=[i0], chain=False)
+    ms(T.mu4[:, 0:C:4], 0.0)
+    ms(T.z[:, C:C + 3], 256.0, chain=False)
+    ms(T.dbl[:, 0:528:88], -1024.0, chain=False)
+    cp(T.rcol[:, 0:1], T.rint[:, 0:1], chain=False)
+    uoff = cp(T.uoff[:], T.ui[:], after=[i2], chain=False, sig="c0")
+    ts(T.t32[:], T.j32[:], T.rcol[:, 0:1], A.subtract, after=[i1])
+    ts(T.pw[:, 0:K], T.k16[:, 0:K], T.rcol[:, 0:1], A.add, after=[i3], chain=False)
+    ts(T.bcol[:, 0:1], T.rcol[:, 0:1], 14.5, A.is_lt, 1024.0, A.mult, chain=False)
+    ms(T.tab0[:], 1000.0, chain=False)
+    ts(T.ca[:], T.t32[:], 4.0, A.is_equal, 65532.0, A.mult)
+    ts(T.cb[:], T.t32[:], 0.0, A.is_equal, -4.0, A.mult, chain=False)
+    ts(T.cc[:], T.t32[:], 4.0, A.is_le, 3.0, A.mult, chain=False)
+    ts(T.cf[:], T.t32[:, 0:16], 1.0, A.is_equal, chain=False)
+    ts(T.th0[:, 0:6], T.pw[:, 0:6], -1.0, A.mult, 87.0, A.add, chain=False)
+    ts(T.th1[:, 0:6], T.pw[:, 0:6], 87.5, A.is_gt, -1000.0, A.mult, chain=False)
+    ts(T.dump[:, 0:6], T.pw[:, 0:6], 257.0, A.add, chain=False)
+    ts(T.c352[:, 0:K], T.pw[:, 0:K], float(C), A.add, chain=False)
+    tt(T.cd[:], T.ca[:], T.cb[:], A.add)
+    tt(T.cg[:], T.cb[:, 0:16], T.cf[:], A.add, chain=False)
+    tt(T.thm[:, 0:6], T.th0[:, 0:6], T.th1[:, 0:6], A.add, chain=False)
+    c1 = tt(T.ce[:], T.cd[:], T.cc[:], A.add, sig="c1")
+    ms(T.et[:], 0.0, chain=False)
+    act(T.mu32[:, 0:32], T.ce[:], F.Identity, bias=1.0, after=[c1])
+    act(T.m16[:, 0:16], T.cg[:], F.Identity, scale=-1.0, chain=False)
+    act(T.mu32[:, 32:64], T.mu32[:, 0:32], F.Copy)
+    act(T.m16[:, 16:32], T.m16[:, 0:16], F.Copy, chain=False)
+    act(T.mu32[:, 64:128], T.mu32[:, 0:64], F.Copy)
+    act(T.m16[:, 32:64], T.m16[:, 0:32], F.Copy, chain=False)
+    act(T.mu32[:, 128:256], T.mu32[:, 0:128], F.Copy)
+    act(T.m16[:, 64:128], T.m16[:, 0:64], F.Copy, chain=False)
+    cmu = act(T.mu32[:, 256:C], T.mu32[:, 0:96], F.Copy, sig="c2")
+    cmb = act(T.mb[:], T.m16[:, 0:96], F.Identity, scale=1024.0, chain=False, sig="c3")
+    act(T.m16[:, 128:256], T.m16[:, 0:128], F.Copy, chain=False)
+
+    qu = quant(T.qu[:], T.su[:], T.uin[:], after=[ldu], chain=False, sig="c4")
+    pq = cp(T.qup[:].bitcast(dt.uint32), T.qu[:].bitcast(dt.uint32).indirect(T.uoff[:]), after=[qu, uoff],
+            chain=False, sig="c5")
+    ps = act(T.sup[:], T.su[:].indirect(T.uoff[:]), F.Copy, after=[qu, uoff], chain=False, sig="c6")
+    cm16 = act(T.m16[:, 256:C], T.m16[:, 0:96], F.Copy, sig="c7")
+    for b in range(4):
+        plane = act(T.pl0[:, PL * b:PL * b + C], T.xin[:, b:4 * C:4], F.Identity, scale=64.0, after=[ldx],
+                    chain=False, sig="pl")
+    qx = quant(T.qx0[:], T.sx0[:], T.xin[:], after=[ldx], chain=False, sig="qx")
+
+    tabs = {}
+    w = cmu
+    for t in range(3):
+        mate = T.cores[rank ^ (1 << t)]
+        qX, sX, lq, ls = T["qx%d" % t], T["sx%d" % t], T["lq%d" % t], T["ls%d" % t]
+        lw, ow, pl, pn, tab = T["lw%d" % t], T["ow%d" % t], T["pl%d" % t], T["pl%d" % ((t + 1) % 3)], T["tab%d" % t]
+        a_s = send(mate, ls[:], sX[:], "as%d" % t, [qx])
+        sa = mm(T.psa[:, 0:C], T.qup[:, 0:128], T.sup[:, 0:128], qX[:], sX[:], after=[qx, pq, ps], sig="sa")
+        sb = mm(T.psa[:, 512:512 + C], T.qup[:, 128:256], T.sup[:, 128:256], qX[:], sX[:], sig="sb")
+        ts(T.za[:], T.psa[:, 0:C], 0.0, A.is_gt, 2.0, A.mult, after=[w, sa])
+        ts(T.zb[:], T.psa[:, 512:512 + C], 0.0, A.is_gt, after=[sb], chain=False)
+        tt(T.z[:, 0:C], T.za[:], T.zb[:], A.add)
+        scan(T.w2[:, 0:C], T.mu32[:], T.z[:, 0:C], 0.0, A.mult, A.add)
+        scan(T.w2[:, C:PL], T.mu32[:], T.z[:, 16:16 + C], 0.0, A.mult, A.add, chain=False)
+        ts(ow[:, 0:K:2], T.w2[:, 31:C:32], 2.0 ** -16, A.mult, 256.0, A.min, sig="w")
+        w = ts(ow[:, 1:K:2], T.w2[:, C + 31:PL:32], 2.0 ** -16, A.mult, 256.0, A.min, chain=False, sig="w")
+        a_w = send(mate, lw[:], ow[:], "aw%d" % t, [w])
+        a_q = send(mate, u8(lq[:]), u8(qX[:]), "aq%d" % t, [])
+        if t == 0:
+            for n in (1, 2):
+                tabs[n] = iota(T["tab%d" % n][:], [[0, 360]], 1000, 0, "tb")
+        scan(T.bs[:, 0:C], T.mu4[:], T.z[:, 0:C], 0.0, A.mult, A.add, chain=False)
+        scan(T.be[:], T.mb[:], T.bs[:, 3:384:4], 0.0, A.add, A.min, after=[cmb])
+        ts(T.bw[:, 0:6], T.be[:, 15:96:16], T.bcol[:, 0:1], A.add)
+        for k in range(6):
+            ts(T.eq[:, 88 * k:88 * k + 88], T.bs[:, 3:C:4], T.bw[:, k:k + 1], A.not_equal, -128.0, A.mult, chain=k == 0)
+        scan(T.fs[:], T.dbl[:], T.eq[:], 0.0, A.add, A.max)
+        tt(T.dup[:, 0:6], T.fs[:, 87:528:88], T.thm[:, 0:6], A.is_gt)
+        tt(T.dd[:, 0:6], T.dup[:, 0:6], T.dump[:, 0:6], A.mult)
+        tt(T.so[:, 0:6], T.dd[:, 0:6], T.bw[:, 0:6], A.max)
+        cp(T.soff[:, 0:6], T.so[:, 0:6])
+        tb = cp(tab[:].indirect(T.soff[:, 0:6]), T.vals[:], after=[i4] + ([tabs[2]] if t else []), sig="tab")
+        ts(T.gtab[:, 0:258], tab[:, 0:258], 999.0, A.is_ge, after=[tb])
+        if t == 0:
+            for b in range(4):
+                ts(T.et[:, 512 * b + b:512 * b + 512:4], T.idn[:], 0.0, A.is_equal, after=[i5], chain=False)
+            ms(T.inc[:], 1.0, chain=False)
+            ms(T.ones[:], 1.0, chain=False)
+            ms(T.px[:, 0:1], 4.0, chain=False)
+            ms(T.d[:, 0:1], 0.0, chain=False)
+            ms(T.gm[:, 0:1], 2.5, chain=False)
+            ms(T.nl[:, 0:1], 0.0, chain=False)
+            ms(T.hf[:, K:32], 0.0, chain=False)
+            ms(T.inc[:, 0:C:4], -3.0)
+            qe = quant(T.qe[:], T.se[:], T.et[:], chain=False, sig="qe")
+        if t == 1:
+            qv = quant(T.qv[:], T.sv[:], T.vin[:], after=[ldv], chain=False, sig="qv")
+        val = act(T.val[:], tab[:].indirect(lw[:]), F.Identity, scale=EPS, after=[tb, a_w], chain=False, sig="val")
+        tt(T.px[:, 1:C + 1], T.gtab[:, 0:258].indirect(lw[:]), T.alpha[:], A.mult, after=[a_w, i6])
+        scan(T.py[:], T.px[:, 0:C], T.px[:, 1:C + 1], 0.0, A.max, A.subtract)
+        ts(T.e1[:], T.py[:], 0.0, A.is_gt, 4.0, A.mult)
+        ts(T.e2[:], T.py[:], 4.0, A.min, chain=False)
+        pd = tt(T.pd[:], T.e1[:], T.e2[:], A.subtract, sig="pd")
+        phi = act(T.phi[:], T.pd[:], F.Identity, bias=12.0, scale=-4.0, after=[pd], chain=False, sig="phi")
+        ts(T.keep[:], T.pd[:], 1.5, A.is_lt, after=[pd])
+        scan(T.d[:, 1:C + 1], T.keep[:], T.pd[:], 0.0, A.mult, A.add)
+        ts(T.q[:], T.d[:, 0:C], 1.0 / 3.0, A.mult, 160.0 - 2.0 / 3.0, A.add)
+        ts(T.q[:], T.q[:], -3.0, A.mult, 480.0, A.add)
+        tt(T.pj[:], T.d[:, 0:C], T.q[:], A.add)
+        pv = tt(T.pv[:], T.pj[:], T.phi[:], A.add, after=[phi], sig="pv")
+        v2 = act(T.v2[:], T.pv[:], F.Identity, bias=2.0, after=[pv], chain=False, sig="v2")
+        ts(T.e1[:], T.pv[:], GRID, A.add, GRID + 8.0, A.is_equal, after=[pv])
+        ts(T.e2[:], T.pv[:], GRID, A.add, GRID + 4.0, A.is_equal, chain=False)
+        ts(T.pa[:], T.e1[:], -2.0, A.mult, 1.0, A.add)
+        ts(T.rst[:], T.e2[:], 5.0, A.mult, -2.5, A.add, chain=False)
+        scan(T.gm[:, 1:C + 1], T.pa[:], T.rst[:], 2.5, A.mult, A.max)
+        tt(T.pz[:], T.v2[:], T.gm[:, 0:C], A.add, after=[v2])
+        ts(T.nl[:, 1:C + 1], T.pz[:], GRID, A.add, GRID + 8.0, A.not_equal)
+        scan(T.st[:], T.inc[:], T.nl[:, 0:C], 0.0, A.add, A.mult)
+        cn = scan(T.cnt[:], T.ones[:], T.nl[:, 1:C + 1], 0.0, A.add, A.subtract, chain=False, sig="cnt")
+        for b in range(4):
+            dm = mm(T.psr[:, 512 * b:512 * b + C], T.qe[:, 128 * b:128 * b + 128], T.se[:, 128 * b:128 * b + 128],
+                    lq[:], ls[:], after=[qe, a_s, a_q], sig="dm%d" % b)
+            dcp = act(pl[:, PL * b + C:PL * b + PL], T.psr[:, 512 * b:512 * b + C], F.Identity, scale=64.0,
+                      after=[dm], chain=False, sig="dcp")
+        act(T.sgn[:], T.cnt[:], F.Sign, bias=128.5, scale=-1.0, acc=T.acc[:, 0:1], after=[cn])
+        thr = act(T.thr[:, 0:1], T.acc[:, 0:1], F.Identity, bias=528.0, scale=0.5, sig="thr")
+        ts(T.d0[:], T.st[:], 0.0, A.is_equal, -1023.0 * EPS, A.add)
+        scan(T.hh[:], T.d0[:], T.val[:], 0.0, A.add, A.min, after=[val])
+        scan(T.he[:], T.m16[:], T.hh[:], 0.0, A.add, A.min, after=[cm16])
+        ts(T.hi[:, 0:K], T.he[:, 15:C:16], 1.0 / EPS, A.mult, 2.0 / EPS, A.add)
+        ts(T.hj[:, 0:K], T.hi[:, 0:K], 1023, A.bitwise_and)
+        tt(T.h1[:, 0:K], T.hj[:, 0:K], T.c352[:, 0:K], A.min)
+        ts(T.hu[:, 0:K], T.h1[:, 0:K], T.thr[:, 0:1], A.is_ge, -float(C), A.mult, after=[thr])
+        tt(T.hf[:, 0:K], T.h1[:, 0:K], T.hu[:, 0:K], A.add)
+        off = cp(T.off[:, 0:K], T.hf[:, 0:K], sig="off")
+        pre = [off, dcp] + ([plane] if t == 0 else [])
+        for b in (0, 1):
+            gv = ts(T.gt[:, b:4 * C:4], pl[:, PL * b:PL * b + PL].indirect(T.off[:, 0:K]), 0.015625, A.mult,
+                    after=pre, chain=False, sig="gv")
+        for b in (2, 3):
+            gs = act(T.gt[:, b:4 * C:4], pl[:, PL * b:PL * b + PL].indirect(T.off[:, 0:K]), F.Identity, scale=0.015625,
+                     after=pre, chain=False, sig="gs")
+        qg = quant(T.qg[:], T.sg[:], T.gt[:], after=[gv, gs], chain=False, sig="qg")
+        if t == 2:
+            ht = op("V", lambda: V.transpose(T.ht[:], T.hf[:]), chain=False, sig="ht")
+            for n in range(8):
+                dma("Y", T.ot[n, :], T.ht[32 * (n // 2):32 * (n // 2) + K, 16 * (n % 2):16 * (n % 2) + 16],
+                    "sto", after=[ht])
+        ys = []
+        for b in range(4):
+            r = mm(T.psr[:, 512 * b:512 * b + C], T.qw[:, 128 * b:128 * b + 128], T.sw[:, 128 * b:128 * b + 128],
+                   T.qg[:], T.sg[:], after=[qg, ldw], sig="r%d" % b)
+            gb = act(T.g64[:, C * b:C * b + C], T.gt[:, b:4 * C:4], F.Identity, scale=64.0, after=[gv, gs],
+                     chain=False, sig="gb%d" % b)
+            ys.append(tt(pn[:, PL * b:PL * b + C], T.psr[:, 512 * b:512 * b + C], T.g64[:, C * b:C * b + C], A.add,
+                         after=[r, gb], chain=False, sig="ya%d" % b))
+        for b in (0, 1):
+            xs = act(T.xt[:, b:4 * C:4], pn[:, PL * b:PL * b + C], F.Identity, scale=0.015625, after=[ys[b]],
+                     chain=False, sig="xs")
+        for b in (2, 3):
+            ts(T.xt[:, b:4 * C:4], pn[:, PL * b:PL * b + C], 0.015625, A.mult, after=[ys[b]], chain=False)
+        qx = quant(T["qx%d" % (t + 1)][:], T["sx%d" % (t + 1)][:], T.xt[:], after=[xs], sig="qx")
+
+    ym = mm(T.psa[:, 0:C], T.qv[:], T.sv[:], T.qx3[:], T.sx3[:], after=[qx, qv], sig="ym")
+    dma("Y", T.oc[:], u8(T.qx3[:]), "stc", after=[qx])
+    for k in range(4):
+        dma("S" if k % 2 else "Y", T.osc[4 * k:4 * k + 4, :], T.sx3[32 * k:32 * k + 4, :], "stc", after=[qx])
+    yc = cp(T.yb[:], T.psa[:, 0:C], after=[ym], sig="yc")
+    dma("S", T.y[:], T.yb[:], "sty", after=[yc])
+    for name in cnt:
+        if max(seen[e].get(name, 0) for e in seen) < cnt[name]:
+            wait("G", (name, cnt[name]))

@@ -2,7 +2,7 @@ from concourse.mybir import dt, AluOpType as A, ActivationFunctionType as F
 
 C = 352
 K = C // 16
-PL = 2 * C
+PL = 3 * C
 Q4, U8, BF, F32, I32, U16 = "float8_e4m3fn_x4", "uint8", "bfloat16", "float32", "int32", "uint16"
 
 
@@ -19,21 +19,21 @@ SCRATCH = {
     "yb": _sb(C, F32),
     "pcol": _sb(4, I32), "rint": _sb(4, I32), "rcol": _sb(4, F32), "bcol": _sb(4, F32), "j32": _sb(32, F32),
     "t32": _sb(32, F32), "ca": _sb(32, F32), "cb": _sb(32, F32), "cc": _sb(32, F32), "cd": _sb(32, F32),
-    "ce": _sb(32, F32), "cf": _sb(16, F32), "cg": _sb(16, F32),
-    "ui": _sb(16, I32), "uoff": _sb(16, U16), "k16": _sb(24, F32), "pw": _sb(24, F32), "c352": _sb(24, F32),
+    "ce": _sb(32, F32), "cf": _sb(16, F32), "cg": _sb(16, F32), "hcol": _sb(4, F32),
+    "ui": _sb(16, I32), "uoff": _sb(16, U16), "k16": _sb(24, F32), "pw": _sb(24, F32), "pw2": _sb(24, F32),
     "th0": _sb(8, F32), "th1": _sb(8, F32), "thm": _sb(8, F32), "dump": _sb(8, F32), "idn": _sb(128, F32),
-    "vals": _sb(96, F32), "alpha": _sb(C, BF), "mu32": _sb(C, BF), "mu4": _sb(C, BF), "m16": _sb(C, BF),
-    "mb": _sb(96, BF), "dbl": _sb(528, BF), "ones": _sb(C, BF), "inc": _sb(C, BF),
-    "za": _sb(C, BF), "zb": _sb(C, BF), "z": _sb(368, BF), "w2": _sb(PL, BF), "bs": _sb(384, BF),
+    "vi": _sb(96, F32), "vals": _sb(96, F32), "alpha": _sb(C, BF), "mu32": _sb(C, BF), "mu4": _sb(C, BF),
+    "m16": _sb(C, BF), "mb": _sb(96, BF), "dbl": _sb(528, BF), "ones": _sb(C, BF), "inc": _sb(C, BF),
+    "za": _sb(C, BF), "zb": _sb(C, BF), "z": _sb(368, BF), "w2": _sb(2 * C, BF), "bs": _sb(384, BF),
     "be": _sb(96, F32), "bw": _sb(8, F32), "eq": _sb(528, BF), "fs": _sb(528, BF), "dup": _sb(8, F32),
-    "dd": _sb(8, F32), "so": _sb(8, F32), "soff": _sb(8, U16), "gtab": _sb(272, BF),
+    "so": _sb(8, F32), "soff": _sb(8, U16),
     "px": _sb(368, BF), "py": _sb(C, BF), "pd": _sb(C, BF), "keep": _sb(C, BF),
-    "d": _sb(368, BF), "q": _sb(C, BF), "pj": _sb(C, BF), "phi": _sb(C, BF), "pv": _sb(C, BF),
+    "d": _sb(368, BF), "q": _sb(C, BF), "q3": _sb(C, BF), "pj": _sb(C, BF), "phi": _sb(C, BF), "pv": _sb(C, BF),
     "v2": _sb(C, BF), "e1": _sb(C, BF), "e2": _sb(C, BF), "pa": _sb(C, BF), "rst": _sb(C, BF), "gm": _sb(368, BF),
     "pz": _sb(C, BF), "nl": _sb(368, BF), "cnt": _sb(C, BF), "sgn": _sb(C, BF), "acc": _sb(4, F32),
-    "thr": _sb(4, F32), "st": _sb(C, BF), "d0": _sb(C, F32), "val": _sb(C, F32), "hh": _sb(C, F32),
+    "st": _sb(C, BF), "d0": _sb(C, BF), "val": _sb(C, F32), "hh": _sb(C, F32),
     "he": _sb(C, F32), "hi": _sb(24, I32), "hj": _sb(24, I32), "h1": _sb(24, F32), "hu": _sb(24, F32),
-    "hf": _sb(32, F32), "ht": _sb(32, F32), "off": _sb(24, U16),
+    "hf": _sb(24, F32), "ho": _sb(32, F32), "ht": _sb(32, F32), "off": _sb(24, U16),
     "psa": ("psum", [128, 1024], F32), "psr": ("psum", [128, 2048], F32),
 }
 for _t in range(4):
@@ -49,12 +49,13 @@ for _t in range(3):
 
 SEMAPHORES = (["V", "S", "T", "G", "ldx", "ldu", "ldw", "ldv", "stc", "sty", "sto", "sent",
                "i0", "i1", "i2", "i3", "i4", "i5", "i6", "tb", "c0", "c1", "c2", "c3", "c4", "c5", "c6", "c7", "c8",
-               "qx", "sa", "sb", "w", "tab", "val", "pd", "phi", "pv", "v2", "cnt", "thr", "off", "gv", "gs", "qg",
-               "xs", "dcp", "qe", "qv", "ym", "yc", "ht", "pl"]
+               "qx", "sa", "sb", "w", "tab", "val", "pd", "phi", "pv", "v2", "cnt", "acc", "off", "gv", "gs", "qg",
+               "xs", "dcp", "qe", "qv", "ym", "yc", "ht", "pl", "d", "q3", "tb0"]
               + ["%s%d" % (n, b) for n in ("r", "dm", "gb", "ya") for b in range(4)]
               + ["%s%d" % (n, t) for n in ("as", "aw", "aq") for t in range(3)])
 
-EPS = 2.0 ** -13
+EPS = 2.0 ** -15
+TINY = 2.0 ** -40
 GRID = 2.0 ** 25
 
 
@@ -136,7 +137,7 @@ def rank_program(g, core, T, topo):
 
     ldu = dma("S", T.uin[:], T.u[:], "ldu")
     ldx = dma("Y", T.xin[:], T.x[:], "ldx")
-    dma("Y", u8(T.qw[:]), T.wc[:], "ldw")
+    dma("Y", u8(T.qw[:]), T.wc[:], "ldw", after=[ldx])
     ldw = dma("Y", T.sw[:], T.ws[:], "ldw")
     ldv = dma("Y", T.vin[:], T.v[:], "ldv")
 
@@ -144,61 +145,61 @@ def rank_program(g, core, T, topo):
     i1 = iota(T.j32[:], [[1, 32]], 0, 0, "i1")
     i2 = iota(T.ui[:], [[1, 2], [16, 8]], 0, 0, "i2", False)
     i3 = iota(T.k16[:, 0:K], [[16, K]], 0, 0, "i3")
-    i4 = iota(T.vals[:], [[4, 96]], 0, 0, "i4")
+    i4 = iota(T.vi[:], [[-4, 96]], 0, 0, "i4")
     i5 = iota(T.idn[:], [[-1, 128]], 0, 1, "i5")
     i6 = iota(T.alpha[:], [[0, C // 4], [-1, 4]], 7, 0, "i6")
+    tabs = {0: iota(T.tab0[:], [[0, 360]], 8, 0, "tb0")}
 
     ms(T.mu4[:], 4.0)
     ms(T.z[:, C:368], 0.0, chain=False)
-    ms(T.bs[:, C:384], 0.0, chain=False)
-    ms(T.dbl[:], 1.0, chain=False)
     ts(T.rint[:, 0:1], T.pcol[:, 0:1], 15, A.bitwise_and, after=[i0], chain=False)
-    ms(T.mu4[:, 0:C:4], 0.0)
+    cp(T.rcol[:, 0:1], T.rint[:, 0:1])
+    ms(T.mu4[:, 0:C:4], 0.0, chain=False)
     ms(T.z[:, C:C + 3], 256.0, chain=False)
-    ms(T.dbl[:, 0:528:88], -1024.0, chain=False)
-    cp(T.rcol[:, 0:1], T.rint[:, 0:1], chain=False)
     uoff = cp(T.uoff[:], T.ui[:], after=[i2], chain=False, sig="c0")
     ts(T.t32[:], T.j32[:], T.rcol[:, 0:1], A.subtract, after=[i1])
     ts(T.pw[:, 0:K], T.k16[:, 0:K], T.rcol[:, 0:1], A.add, after=[i3], chain=False)
     ts(T.bcol[:, 0:1], T.rcol[:, 0:1], 14.5, A.is_lt, 1024.0, A.mult, chain=False)
-    ms(T.tab0[:], 1000.0, chain=False)
     ts(T.ca[:], T.t32[:], 4.0, A.is_equal, 65532.0, A.mult)
     ts(T.cb[:], T.t32[:], 0.0, A.is_equal, -4.0, A.mult, chain=False)
     ts(T.cc[:], T.t32[:], 4.0, A.is_le, 3.0, A.mult, chain=False)
     ts(T.cf[:], T.t32[:, 0:16], 1.0, A.is_equal, chain=False)
-    ts(T.th0[:, 0:6], T.pw[:, 0:6], -1.0, A.mult, 87.0, A.add, chain=False)
-    ts(T.th1[:, 0:6], T.pw[:, 0:6], 87.5, A.is_gt, -1000.0, A.mult, chain=False)
-    ts(T.dump[:, 0:6], T.pw[:, 0:6], 257.0, A.add, chain=False)
-    ts(T.c352[:, 0:K], T.pw[:, 0:K], float(C), A.add, chain=False)
     tt(T.cd[:], T.ca[:], T.cb[:], A.add)
     tt(T.cg[:], T.cb[:, 0:16], T.cf[:], A.add, chain=False)
-    tt(T.thm[:, 0:6], T.th0[:, 0:6], T.th1[:, 0:6], A.add, chain=False)
+    ts(T.th0[:, 0:6], T.pw[:, 0:6], -1.0, A.mult, 87.0, A.add, chain=False)
+    ts(T.th1[:, 0:6], T.pw[:, 0:6], 87.5, A.is_gt, -1000.0, A.mult, chain=False)
     c1 = tt(T.ce[:], T.cd[:], T.cc[:], A.add, sig="c1")
-    ms(T.et[:], 0.0, chain=False)
+    tt(T.thm[:, 0:6], T.th0[:, 0:6], T.th1[:, 0:6], A.add, chain=False)
+    ms(T.bs[:, C:384], 0.0, chain=False)
+    ms(T.dbl[:], 1.0, chain=False)
+    ts(T.dump[:, 0:6], T.pw[:, 0:6], 257.0, A.add, chain=False)
+    ts(T.vals[:], T.vi[:], TINY, A.mult, after=[i4], chain=False)
     act(T.mu32[:, 0:32], T.ce[:], F.Identity, bias=1.0, after=[c1])
     act(T.m16[:, 0:16], T.cg[:], F.Identity, scale=-1.0, chain=False)
     act(T.mu32[:, 32:64], T.mu32[:, 0:32], F.Copy)
     act(T.m16[:, 16:32], T.m16[:, 0:16], F.Copy, chain=False)
     act(T.mu32[:, 64:128], T.mu32[:, 0:64], F.Copy)
     act(T.m16[:, 32:64], T.m16[:, 0:32], F.Copy, chain=False)
-    act(T.mu32[:, 128:256], T.mu32[:, 0:128], F.Copy)
-    act(T.m16[:, 64:128], T.m16[:, 0:64], F.Copy, chain=False)
-    cmu = act(T.mu32[:, 256:C], T.mu32[:, 0:96], F.Copy, sig="c2")
-    cmb = act(T.mb[:], T.m16[:, 0:96], F.Identity, scale=1024.0, chain=False, sig="c3")
-    act(T.m16[:, 128:256], T.m16[:, 0:128], F.Copy, chain=False)
 
     qu = quant(T.qu[:], T.su[:], T.uin[:], after=[ldu], chain=False, sig="c4")
     pq = cp(T.qup[:].bitcast(dt.uint32), T.qu[:].bitcast(dt.uint32).indirect(T.uoff[:]), after=[qu, uoff],
             chain=False, sig="c5")
     ps = act(T.sup[:], T.su[:].indirect(T.uoff[:]), F.Copy, after=[qu, uoff], chain=False, sig="c6")
-    cm16 = act(T.m16[:, 256:C], T.m16[:, 0:96], F.Copy, sig="c7")
+    act(T.mu32[:, 128:256], T.mu32[:, 0:128], F.Copy)
+    act(T.mu32[:, 256:C], T.mu32[:, 0:96], F.Copy, chain=False)
+    act(T.m16[:, 64:128], T.m16[:, 0:64], F.Copy, chain=False)
+    cmb = act(T.mb[:], T.m16[:, 0:96], F.Identity, scale=1024.0, sig="c3")
+    act(T.m16[:, 128:256], T.m16[:, 0:128], F.Copy, chain=False, sig="c7")
+    cm16 = act(T.m16[:, 256:C], T.m16[:, 0:96], F.Copy, chain=False, sig="c7")
     for b in range(4):
-        plane = act(T.pl0[:, PL * b:PL * b + C], T.xin[:, b:4 * C:4], F.Identity, scale=64.0, after=[ldx],
-                    chain=False, sig="pl")
+        for at in (0, 2 * C):
+            plane = act(T.pl0[:, PL * b + at:PL * b + at + C], T.xin[:, b:4 * C:4], F.Identity, scale=64.0,
+                        after=[ldx], chain=False, sig="pl")
     qx = quant(T.qx0[:], T.sx0[:], T.xin[:], after=[ldx], chain=False, sig="qx")
+    ms(T.dbl[:, 0:528:88], -1024.0)
+    ms(T.et[:, 0:1024], 0.0, chain=False)
 
-    tabs = {}
-    w = cmu
+    w = cmb
     for t in range(3):
         mate = T.cores[rank ^ (1 << t)]
         qX, sX, lq, ls = T["qx%d" % t], T["sx%d" % t], T["lq%d" % t], T["ls%d" % t]
@@ -206,30 +207,32 @@ def rank_program(g, core, T, topo):
         a_s = send(mate, ls[:], sX[:], "as%d" % t, [qx])
         sa = mm(T.psa[:, 0:C], T.qup[:, 0:128], T.sup[:, 0:128], qX[:], sX[:], after=[qx, pq, ps], sig="sa")
         sb = mm(T.psa[:, 512:512 + C], T.qup[:, 128:256], T.sup[:, 128:256], qX[:], sX[:], sig="sb")
-        ts(T.za[:], T.psa[:, 0:C], 0.0, A.is_gt, 2.0, A.mult, after=[w, sa])
+        ts(T.za[:], T.psa[:, 0:C], 0.0, A.is_gt, 2.0, A.mult, after=[sa], chain=False)
         ts(T.zb[:], T.psa[:, 512:512 + C], 0.0, A.is_gt, after=[sb], chain=False)
-        tt(T.z[:, 0:C], T.za[:], T.zb[:], A.add)
+        tt(T.z[:, 0:C], T.za[:], T.zb[:], A.add, after=[w])
         scan(T.w2[:, 0:C], T.mu32[:], T.z[:, 0:C], 0.0, A.mult, A.add)
-        scan(T.w2[:, C:PL], T.mu32[:], T.z[:, 16:16 + C], 0.0, A.mult, A.add, chain=False)
+        scan(T.w2[:, C:2 * C], T.mu32[:], T.z[:, 16:16 + C], 0.0, A.mult, A.add, chain=False)
+        scan(T.bs[:, 0:C], T.mu4[:], T.z[:, 0:C], 0.0, A.mult, A.add, chain=False, sig="c8")
         ts(ow[:, 0:K:2], T.w2[:, 31:C:32], 2.0 ** -16, A.mult, 256.0, A.min, sig="w")
-        w = ts(ow[:, 1:K:2], T.w2[:, C + 31:PL:32], 2.0 ** -16, A.mult, 256.0, A.min, chain=False, sig="w")
+        w = ts(ow[:, 1:K:2], T.w2[:, C + 31:2 * C:32], 2.0 ** -16, A.mult, 256.0, A.min, chain=False, sig="w")
         a_w = send(mate, lw[:], ow[:], "aw%d" % t, [w])
         a_q = send(mate, u8(lq[:]), u8(qX[:]), "aq%d" % t, [])
         if t == 0:
             for n in (1, 2):
-                tabs[n] = iota(T["tab%d" % n][:], [[0, 360]], 1000, 0, "tb")
-        scan(T.bs[:, 0:C], T.mu4[:], T.z[:, 0:C], 0.0, A.mult, A.add, chain=False)
-        scan(T.be[:], T.mb[:], T.bs[:, 3:384:4], 0.0, A.add, A.min, after=[cmb])
+                tabs[n] = iota(T["tab%d" % n][:], [[0, 360]], 8, 0, "tb")
+            tabs[1] = tabs[2]
+        scan(T.be[:], T.mb[:], T.bs[:, 3:384:4], 0.0, A.add, A.min, after=[("c8", t + 1)], chain=False)
         ts(T.bw[:, 0:6], T.be[:, 15:96:16], T.bcol[:, 0:1], A.add)
         for k in range(6):
             ts(T.eq[:, 88 * k:88 * k + 88], T.bs[:, 3:C:4], T.bw[:, k:k + 1], A.not_equal, -128.0, A.mult, chain=k == 0)
         scan(T.fs[:], T.dbl[:], T.eq[:], 0.0, A.add, A.max)
         tt(T.dup[:, 0:6], T.fs[:, 87:528:88], T.thm[:, 0:6], A.is_gt)
-        tt(T.dd[:, 0:6], T.dup[:, 0:6], T.dump[:, 0:6], A.mult)
-        tt(T.so[:, 0:6], T.dd[:, 0:6], T.bw[:, 0:6], A.max)
+        tt(T.dup[:, 0:6], T.dup[:, 0:6], T.dump[:, 0:6], A.mult)
+        tt(T.so[:, 0:6], T.dup[:, 0:6], T.bw[:, 0:6], A.max)
         cp(T.soff[:, 0:6], T.so[:, 0:6])
-        tb = cp(tab[:].indirect(T.soff[:, 0:6]), T.vals[:], after=[i4] + ([tabs[2]] if t else []), sig="tab")
-        ts(T.gtab[:, 0:258], tab[:, 0:258], 999.0, A.is_ge, after=[tb])
+        if t == 0:
+            ms(T.et[:, 1024:2048], 0.0, chain=False)
+        tb = cp(tab[:].indirect(T.soff[:, 0:6]), T.vals[:], after=[tabs[t]], sig="tab")
         if t == 0:
             for b in range(4):
                 ts(T.et[:, 512 * b + b:512 * b + 512:4], T.idn[:], 0.0, A.is_equal, after=[i5], chain=False)
@@ -239,26 +242,29 @@ def rank_program(g, core, T, topo):
             ms(T.d[:, 0:1], 0.0, chain=False)
             ms(T.gm[:, 0:1], 2.5, chain=False)
             ms(T.nl[:, 0:1], 0.0, chain=False)
-            ms(T.hf[:, K:32], 0.0, chain=False)
+            ms(T.ho[:, K:32], 0.0, chain=False)
+            ts(T.pw2[:, 0:K], T.pw[:, 0:K], 2.0, A.mult, -float(C), A.add, chain=False)
+            ts(T.hcol[:, 0:1], T.bcol[:, 0:1], 32760.0 / 1024.0, A.mult, 16384.0, A.add, chain=False)
             ms(T.inc[:, 0:C:4], -3.0)
             qe = quant(T.qe[:], T.se[:], T.et[:], chain=False, sig="qe")
         if t == 1:
             qv = quant(T.qv[:], T.sv[:], T.vin[:], after=[ldv], chain=False, sig="qv")
-        val = act(T.val[:], tab[:].indirect(lw[:]), F.Identity, scale=EPS, after=[tb, a_w], chain=False, sig="val")
-        tt(T.px[:, 1:C + 1], T.gtab[:, 0:258].indirect(lw[:]), T.alpha[:], A.mult, after=[a_w, i6])
+        val = act(T.val[:], tab[:].indirect(lw[:]), F.Relu, bias=2 * C * EPS, scale=-EPS / TINY, after=[tb, a_w],
+                  chain=False, sig="val")
+        tt(T.px[:, 1:C + 1], tab[:].indirect(lw[:]), T.alpha[:], A.min, after=[tb, a_w, i6], chain=t == 0)
         scan(T.py[:], T.px[:, 0:C], T.px[:, 1:C + 1], 0.0, A.max, A.subtract)
         ts(T.e1[:], T.py[:], 0.0, A.is_gt, 4.0, A.mult)
         ts(T.e2[:], T.py[:], 4.0, A.min, chain=False)
         pd = tt(T.pd[:], T.e1[:], T.e2[:], A.subtract, sig="pd")
         phi = act(T.phi[:], T.pd[:], F.Identity, bias=12.0, scale=-4.0, after=[pd], chain=False, sig="phi")
-        ts(T.keep[:], T.pd[:], 1.5, A.is_lt, after=[pd])
-        scan(T.d[:, 1:C + 1], T.keep[:], T.pd[:], 0.0, A.mult, A.add)
-        ts(T.q[:], T.d[:, 0:C], 1.0 / 3.0, A.mult, 160.0 - 2.0 / 3.0, A.add)
-        ts(T.q[:], T.q[:], -3.0, A.mult, 480.0, A.add)
-        tt(T.pj[:], T.d[:, 0:C], T.q[:], A.add)
-        pv = tt(T.pv[:], T.pj[:], T.phi[:], A.add, after=[phi], sig="pv")
+        ts(T.keep[:], T.pd[:], 1.5, A.is_lt, after=[pd], chain=False)
+        dn = scan(T.d[:, 1:C + 1], T.keep[:], T.pd[:], 0.0, A.mult, A.add, sig="d")
+        act(T.q[:], T.d[:, 0:C], F.Identity, bias=160.0 - 2.0 / 3.0, scale=1.0 / 3.0, after=[dn], chain=False)
+        q3 = act(T.q3[:], T.q[:], F.Identity, bias=480.0, scale=-3.0, sig="q3")
+        tt(T.pj[:], T.d[:, 0:C], T.phi[:], A.add, after=[dn, phi], chain=False)
+        pv = tt(T.pv[:], T.pj[:], T.q3[:], A.add, after=[q3], sig="pv")
         v2 = act(T.v2[:], T.pv[:], F.Identity, bias=2.0, after=[pv], chain=False, sig="v2")
-        ts(T.e1[:], T.pv[:], GRID, A.add, GRID + 8.0, A.is_equal, after=[pv])
+        ts(T.e1[:], T.pv[:], GRID, A.add, GRID + 8.0, A.is_equal, after=[pv], chain=False)
         ts(T.e2[:], T.pv[:], GRID, A.add, GRID + 4.0, A.is_equal, chain=False)
         ts(T.pa[:], T.e1[:], -2.0, A.mult, 1.0, A.add)
         ts(T.rst[:], T.e2[:], 5.0, A.mult, -2.5, A.add, chain=False)
@@ -270,52 +276,63 @@ def rank_program(g, core, T, topo):
         for b in range(4):
             dm = mm(T.psr[:, 512 * b:512 * b + C], T.qe[:, 128 * b:128 * b + 128], T.se[:, 128 * b:128 * b + 128],
                     lq[:], ls[:], after=[qe, a_s, a_q], sig="dm%d" % b)
-            dcp = act(pl[:, PL * b + C:PL * b + PL], T.psr[:, 512 * b:512 * b + C], F.Identity, scale=64.0,
+            dcp = act(pl[:, PL * b + C:PL * b + 2 * C], T.psr[:, 512 * b:512 * b + C], F.Identity, scale=64.0,
                       after=[dm], chain=False, sig="dcp")
-        act(T.sgn[:], T.cnt[:], F.Sign, bias=128.5, scale=-1.0, acc=T.acc[:, 0:1], after=[cn])
-        thr = act(T.thr[:, 0:1], T.acc[:, 0:1], F.Identity, bias=528.0, scale=0.5, sig="thr")
-        ts(T.d0[:], T.st[:], 0.0, A.is_equal, -1023.0 * EPS, A.add)
+        acc = act(T.sgn[:], T.cnt[:], F.Sign, bias=128.5, scale=-1.0, acc=T.acc[:, 0:1], after=[cn], chain=False,
+                  sig="acc")
+        ts(T.d0[:], T.st[:], 0.0, A.is_equal, -4096.0 * EPS, A.add)
         scan(T.hh[:], T.d0[:], T.val[:], 0.0, A.add, A.min, after=[val])
         scan(T.he[:], T.m16[:], T.hh[:], 0.0, A.add, A.min, after=[cm16])
-        ts(T.hi[:, 0:K], T.he[:, 15:C:16], 1.0 / EPS, A.mult, 2.0 / EPS, A.add)
-        ts(T.hj[:, 0:K], T.hi[:, 0:K], 1023, A.bitwise_and)
-        tt(T.h1[:, 0:K], T.hj[:, 0:K], T.c352[:, 0:K], A.min)
-        ts(T.hu[:, 0:K], T.h1[:, 0:K], T.thr[:, 0:1], A.is_ge, -float(C), A.mult, after=[thr])
-        tt(T.hf[:, 0:K], T.h1[:, 0:K], T.hu[:, 0:K], A.add)
+        ts(T.hu[:, 0:K], T.pw2[:, 0:K], T.acc[:, 0:1], A.is_lt, float(C), A.mult, after=[acc], chain=False)
+        ts(T.hi[:, 0:K], T.he[:, 15:C:16], 4095.0 / 4096.0 / EPS, A.mult, T.hcol[:, 0:1], A.add)
+        tt(T.h1[:, 0:K], T.hu[:, 0:K], T.pw[:, 0:K], A.add, chain=False)
+        ts(T.hj[:, 0:K], T.hi[:, 0:K], 4095, A.bitwise_and)
+        tt(T.hf[:, 0:K], T.hj[:, 0:K], T.h1[:, 0:K], A.max)
         off = cp(T.off[:, 0:K], T.hf[:, 0:K], sig="off")
-        pre = [off, dcp] + ([plane] if t == 0 else [])
+        pre = [off, dcp, plane]
         for b in (0, 1):
             gv = ts(T.gt[:, b:4 * C:4], pl[:, PL * b:PL * b + PL].indirect(T.off[:, 0:K]), 0.015625, A.mult,
                     after=pre, chain=False, sig="gv")
         for b in (2, 3):
             gs = act(T.gt[:, b:4 * C:4], pl[:, PL * b:PL * b + PL].indirect(T.off[:, 0:K]), F.Identity, scale=0.015625,
                      after=pre, chain=False, sig="gs")
-        qg = quant(T.qg[:], T.sg[:], T.gt[:], after=[gv, gs], chain=False, sig="qg")
         if t == 2:
-            ht = op("V", lambda: V.transpose(T.ht[:], T.hf[:]), chain=False, sig="ht")
-            for n in range(8):
-                dma("Y", T.ot[n, :], T.ht[32 * (n // 2):32 * (n // 2) + K, 16 * (n % 2):16 * (n % 2) + 16],
-                    "sto", after=[ht])
+            ts(T.hu[:, 0:K], T.hf[:, 0:K], 2.0 * C - 0.5, A.is_gt, -2.0 * C, A.mult, chain=False)
+        qg = quant(T.qg[:], T.sg[:], T.gt[:], after=[gv, gs], chain=False, sig="qg")
+        gb = ts(T.g64[:, 0:C], T.gt[:, 0:4 * C:4], 64.0, A.mult, chain=False, sig="gb0")
+        if t == 2:
+            tt(T.ho[:, 0:K], T.hu[:, 0:K], T.hf[:, 0:K], A.add)
         ys = []
         for b in range(4):
+            at = PL * b + 2 * C
             r = mm(T.psr[:, 512 * b:512 * b + C], T.qw[:, 128 * b:128 * b + 128], T.sw[:, 128 * b:128 * b + 128],
                    T.qg[:], T.sg[:], after=[qg, ldw], sig="r%d" % b)
-            gb = act(T.g64[:, C * b:C * b + C], T.gt[:, b:4 * C:4], F.Identity, scale=64.0, after=[gv, gs],
-                     chain=False, sig="gb%d" % b)
-            ys.append(tt(pn[:, PL * b:PL * b + C], T.psr[:, 512 * b:512 * b + C], T.g64[:, C * b:C * b + C], A.add,
-                         after=[r, gb], chain=False, sig="ya%d" % b))
-        for b in (0, 1):
-            xs = act(T.xt[:, b:4 * C:4], pn[:, PL * b:PL * b + C], F.Identity, scale=0.015625, after=[ys[b]],
+            if b:
+                gb = act(T.g64[:, C * b:C * b + C], T.gt[:, b:4 * C:4], F.Identity, scale=64.0, after=[gv, gs],
+                         chain=False, sig="gb%d" % b)
+            ys.append(tt(pn[:, at:at + C], T.psr[:, 512 * b:512 * b + C], T.g64[:, C * b:C * b + C], A.add,
+                         after=[gb, r], chain=False, sig="ya%d" % b))
+            if t == 2 and b == 0:
+                ht = op("V", lambda: V.transpose(T.ht[:], T.ho[:]), sig="ht")
+                for n in range(8):
+                    dma("Y", T.ot[n, :], T.ht[32 * (n // 2):32 * (n // 2) + K, 16 * (n % 2):16 * (n % 2) + 16],
+                        "sto", after=[ht])
+        for b in range(3):
+            at = PL * b + 2 * C
+            xs = act(T.xt[:, b:4 * C:4], pn[:, at:at + C], F.Identity, scale=0.015625, after=[ys[b]],
                      chain=False, sig="xs")
-        for b in (2, 3):
-            ts(T.xt[:, b:4 * C:4], pn[:, PL * b:PL * b + C], 0.015625, A.mult, after=[ys[b]], chain=False)
+        ts(T.xt[:, 3:4 * C:4], pn[:, PL * 3 + 2 * C:PL * 4], 0.015625, A.mult, after=[ys[3]], chain=False)
         qx = quant(T["qx%d" % (t + 1)][:], T["sx%d" % (t + 1)][:], T.xt[:], after=[xs], sig="qx")
+        if t < 2:
+            for b in range(4):
+                plane = act(pn[:, PL * b:PL * b + C], pn[:, PL * b + 2 * C:PL * b + PL], F.Copy, after=[ys[b]],
+                            chain=False, sig="pl")
 
     ym = mm(T.psa[:, 0:C], T.qv[:], T.sv[:], T.qx3[:], T.sx3[:], after=[qx, qv], sig="ym")
     dma("Y", T.oc[:], u8(T.qx3[:]), "stc", after=[qx])
     for k in range(4):
-        dma("S" if k % 2 else "Y", T.osc[4 * k:4 * k + 4, :], T.sx3[32 * k:32 * k + 4, :], "stc", after=[qx])
-    yc = cp(T.yb[:], T.psa[:, 0:C], after=[ym], sig="yc")
+        dma("Y", T.osc[4 * k:4 * k + 4, :], T.sx3[32 * k:32 * k + 4, :], "stc", after=[qx])
+    yc = cp(T.yb[:], T.psa[:, 0:C], after=[ym], chain=False, sig="yc")
     dma("S", T.y[:], T.yb[:], "sty", after=[yc])
     for name in cnt:
         if max(seen[e].get(name, 0) for e in seen) < cnt[name]:

@@ -3,6 +3,7 @@ from concourse.mybir import dt, AluOpType as A, ActivationFunctionType as F
 C = 352
 K = C // 16
 PL = 3 * C
+HALF = ((0, 160), (160, C))
 Q4, U8, BF, F32, I32, U16 = "float8_e4m3fn_x4", "uint8", "bfloat16", "float32", "int32", "uint16"
 
 
@@ -21,12 +22,12 @@ SCRATCH = {
     "t32": _sb(32, F32), "ca": _sb(32, F32), "cb": _sb(32, F32), "cc": _sb(32, F32), "cd": _sb(32, F32),
     "ce": _sb(32, F32), "cf": _sb(16, F32), "cg": _sb(16, F32), "hcol": _sb(4, F32),
     "ui": _sb(16, I32), "uoff": _sb(16, U16), "k16": _sb(24, F32), "pw": _sb(24, F32), "pw2": _sb(24, F32),
-    "th0": _sb(8, F32), "th1": _sb(8, F32), "thm": _sb(8, F32), "dump": _sb(8, F32), "idn": _sb(128, F32),
+    "th0": _sb(16, F32), "thm": _sb(8, F32), "dump": _sb(8, F32), "idn": _sb(128, F32),
     "vi": _sb(96, F32), "vals": _sb(96, F32), "alpha": _sb(C, BF), "mu32": _sb(C, BF), "mu4": _sb(C, BF),
     "m16": _sb(C, BF), "mb": _sb(96, BF), "dbl": _sb(528, BF), "ones": _sb(C, BF), "inc": _sb(C, BF),
-    "za": _sb(C, BF), "zb": _sb(C, BF), "z": _sb(368, BF), "w2": _sb(2 * C, BF), "bs": _sb(384, BF),
-    "be": _sb(96, F32), "bw": _sb(8, F32), "eq": _sb(528, BF), "fs": _sb(528, BF), "dup": _sb(8, F32),
-    "so": _sb(8, F32), "soff": _sb(8, U16),
+    "za": _sb(368, BF), "zb": _sb(368, BF), "w2": _sb(4 * C, BF), "w22": _sb(24, F32), "bs": _sb(2 * C, BF),
+    "bsum": _sb(96, BF), "be": _sb(96, F32), "bw": _sb(8, F32), "eq": _sb(528, BF), "fs": _sb(528, BF),
+    "dup": _sb(8, F32), "so": _sb(8, F32), "soff": _sb(8, U16),
     "px": _sb(368, BF), "py": _sb(C, BF), "pd": _sb(C, BF), "keep": _sb(C, BF),
     "d": _sb(368, BF), "q": _sb(C, BF), "q3": _sb(C, BF), "pj": _sb(C, BF), "phi": _sb(C, BF), "pv": _sb(C, BF),
     "v2": _sb(C, BF), "e1": _sb(C, BF), "e2": _sb(C, BF), "pa": _sb(C, BF), "rst": _sb(C, BF), "gm": _sb(368, BF),
@@ -47,10 +48,11 @@ for _t in range(3):
     SCRATCH["pl%d" % _t] = _sb(4 * PL, BF)
     SCRATCH["tab%d" % _t] = _sb(360, F32)
 
-SEMAPHORES = (["V", "S", "T", "G", "ldx", "ldu", "ldw", "ldv", "stc", "sty", "sto", "sent",
+SEMAPHORES = (["V", "S", "T", "G", "V1", "S1", "ldx", "ldu", "ldw", "ldv", "stc", "sty", "sto", "sent",
                "i0", "i1", "i2", "i3", "i4", "i5", "i6", "tb", "c0", "c1", "c2", "c3", "c4", "c5", "c6", "c7", "c8",
-               "qx", "sa", "sb", "w", "tab", "val", "pd", "phi", "pv", "v2", "cnt", "acc", "off", "gv", "gs", "qg",
-               "xs", "dcp", "qe", "qv", "ym", "yc", "ht", "pl", "d", "q3", "tb0"]
+               "qx", "sa", "sb", "w", "tab", "acc", "gv", "gs", "qg", "za", "hu", "h1",
+               "xs", "dcp", "qe", "qv", "ym", "yc", "ht", "pl", "tb0"]
+              + ["%s%d" % (n, h) for n in ("val", "pd", "phi", "pv", "vv", "cnt", "off", "d", "qq") for h in range(2)]
               + ["%s%d" % (n, b) for n in ("r", "dm", "gb", "ya") for b in range(4)]
               + ["%s%d" % (n, t) for n in ("as", "aw", "aq") for t in range(3)])
 
@@ -72,12 +74,13 @@ def rank_program(g, core, T, topo):
             queue[e].wait_ge(T.sem[name], n)
             seen[e][name] = n
 
-    def op(e, call, after=(), chain=True, sig=None, inc=1):
-        if chain and cnt.get(e, 0):
-            wait(e, (e, cnt[e]))
+    def op(e, call, after=(), chain=True, sig=None, inc=1, lane=0):
+        own = e + ("1" if lane else "")
+        if chain and cnt.get(own, 0):
+            wait(e, (own, cnt[own]))
         for tok in after:
             wait(e, tok)
-        name = sig or e
+        name = sig or own
         call().then_inc(T.sem[name], inc)
         cnt[name] = cnt.get(name, 0) + inc
         return (name, cnt[name])
@@ -151,11 +154,12 @@ def rank_program(g, core, T, topo):
     tabs = {0: iota(T.tab0[:], [[0, 360]], 8, 0, "tb0")}
 
     ms(T.mu4[:], 4.0)
-    ms(T.z[:, C:368], 0.0, chain=False)
+    ms(T.za[:, C:368], 0.0, chain=False)
+    ms(T.zb[:, C:368], 0.0, chain=False)
     ts(T.rint[:, 0:1], T.pcol[:, 0:1], 15, A.bitwise_and, after=[i0], chain=False)
     cp(T.rcol[:, 0:1], T.rint[:, 0:1])
     ms(T.mu4[:, 0:C:4], 0.0, chain=False)
-    ms(T.z[:, C:C + 3], 256.0, chain=False)
+    ms(T.zb[:, C:C + 3], 256.0, chain=False)
     uoff = cp(T.uoff[:], T.ui[:], after=[i2], chain=False, sig="c0")
     ts(T.t32[:], T.j32[:], T.rcol[:, 0:1], A.subtract, after=[i1])
     ts(T.pw[:, 0:K], T.k16[:, 0:K], T.rcol[:, 0:1], A.add, after=[i3], chain=False)
@@ -167,10 +171,10 @@ def rank_program(g, core, T, topo):
     tt(T.cd[:], T.ca[:], T.cb[:], A.add)
     tt(T.cg[:], T.cb[:, 0:16], T.cf[:], A.add, chain=False)
     ts(T.th0[:, 0:6], T.pw[:, 0:6], -1.0, A.mult, 87.0, A.add, chain=False)
-    ts(T.th1[:, 0:6], T.pw[:, 0:6], 87.5, A.is_gt, -1000.0, A.mult, chain=False)
+    ts(T.th0[:, 8:14], T.pw[:, 0:6], 87.5, A.is_gt, -1000.0, A.mult, chain=False)
     c1 = tt(T.ce[:], T.cd[:], T.cc[:], A.add, sig="c1")
-    tt(T.thm[:, 0:6], T.th0[:, 0:6], T.th1[:, 0:6], A.add, chain=False)
-    ms(T.bs[:, C:384], 0.0, chain=False)
+    tt(T.thm[:, 0:6], T.th0[:, 0:6], T.th0[:, 8:14], A.add, chain=False)
+    ms(T.bsum[:, 88:96], 0.0, chain=False)
     ms(T.dbl[:], 1.0, chain=False)
     ts(T.dump[:, 0:6], T.pw[:, 0:6], 257.0, A.add, chain=False)
     ts(T.vals[:], T.vi[:], TINY, A.mult, after=[i4], chain=False)
@@ -191,52 +195,71 @@ def rank_program(g, core, T, topo):
     cmb = act(T.mb[:], T.m16[:, 0:96], F.Identity, scale=1024.0, sig="c3")
     act(T.m16[:, 128:256], T.m16[:, 0:128], F.Copy, chain=False, sig="c7")
     cm16 = act(T.m16[:, 256:C], T.m16[:, 0:96], F.Copy, chain=False, sig="c7")
-    for b in range(4):
-        for at in (0, 2 * C):
-            plane = act(T.pl0[:, PL * b + at:PL * b + at + C], T.xin[:, b:4 * C:4], F.Identity, scale=64.0,
-                        after=[ldx], chain=False, sig="pl")
     qx = quant(T.qx0[:], T.sx0[:], T.xin[:], after=[ldx], chain=False, sig="qx")
     ms(T.dbl[:, 0:528:88], -1024.0)
-    ms(T.et[:, 0:1024], 0.0, chain=False)
+    ms(T.et[:, 0:512], 0.0, chain=False)
 
     w = cmb
+    ys = []
     for t in range(3):
         mate = T.cores[rank ^ (1 << t)]
         qX, sX, lq, ls = T["qx%d" % t], T["sx%d" % t], T["lq%d" % t], T["ls%d" % t]
         lw, ow, pl, pn, tab = T["lw%d" % t], T["ow%d" % t], T["pl%d" % t], T["pl%d" % ((t + 1) % 3)], T["tab%d" % t]
         a_s = send(mate, ls[:], sX[:], "as%d" % t, [qx])
-        sa = mm(T.psa[:, 0:C], T.qup[:, 0:128], T.sup[:, 0:128], qX[:], sX[:], after=[qx, pq, ps], sig="sa")
-        sb = mm(T.psa[:, 512:512 + C], T.qup[:, 128:256], T.sup[:, 128:256], qX[:], sX[:], sig="sb")
-        ts(T.za[:], T.psa[:, 0:C], 0.0, A.is_gt, 2.0, A.mult, after=[sa], chain=False)
-        ts(T.zb[:], T.psa[:, 512:512 + C], 0.0, A.is_gt, after=[sb], chain=False)
-        tt(T.z[:, 0:C], T.za[:], T.zb[:], A.add, after=[w])
-        scan(T.w2[:, 0:C], T.mu32[:], T.z[:, 0:C], 0.0, A.mult, A.add)
-        scan(T.w2[:, C:2 * C], T.mu32[:], T.z[:, 16:16 + C], 0.0, A.mult, A.add, chain=False)
-        scan(T.bs[:, 0:C], T.mu4[:], T.z[:, 0:C], 0.0, A.mult, A.add, chain=False, sig="c8")
-        ts(ow[:, 0:K:2], T.w2[:, 31:C:32], 2.0 ** -16, A.mult, 256.0, A.min, sig="w")
-        w = ts(ow[:, 1:K:2], T.w2[:, C + 31:2 * C:32], 2.0 ** -16, A.mult, 256.0, A.min, chain=False, sig="w")
+        sb = mm(T.psa[:, 512:512 + C], T.qup[:, 128:256], T.sup[:, 128:256], qX[:], sX[:], after=[qx, pq, ps], sig="sb")
+        sa = mm(T.psa[:, 0:C], T.qup[:, 0:128], T.sup[:, 0:128], qX[:], sX[:], sig="sa")
+        for h, (a, b) in enumerate(HALF):
+            act(T.sgn[:, a:b], T.psa[:, a:b], F.Sign, after=[sa], chain=False, lane=h)
+        for h, (a, b) in enumerate(HALF):
+            za = act(T.za[:, a:b], T.sgn[:, a:b], F.Relu, scale=2.0, lane=h, sig="za")
+        for b in range(4):
+            if t == 0:
+                for at in (0, 2 * C):
+                    plane = act(pl[:, PL * b + at:PL * b + at + C], T.xin[:, b:4 * C:4], F.Identity, scale=64.0,
+                                after=[ldx], chain=False, sig="pl")
+            else:
+                plane = act(pl[:, PL * b:PL * b + C], pl[:, PL * b + 2 * C:PL * b + PL], F.Copy, after=[ys[b]],
+                            chain=False, sig="pl")
+        ts(T.zb[:, 0:C], T.psa[:, 512:512 + C], 0.0, A.is_gt, after=[sb], chain=False)
+        scan(T.w2[:, 0:C], T.mu32[:], T.zb[:, 0:C], 0.0, A.mult, A.add, after=[w])
+        scan(T.w2[:, C:2 * C], T.mu32[:], T.zb[:, 16:16 + C], 0.0, A.mult, A.add, chain=False)
+        scan(T.bs[:, 0:C], T.mu4[:], T.zb[:, 0:C], 0.0, A.mult, A.add, chain=False)
+        scan(T.w2[:, 2 * C:3 * C], T.mu32[:], T.za[:, 0:C], 0.0, A.mult, A.add, after=[za], chain=False)
+        scan(T.w2[:, 3 * C:4 * C], T.mu32[:], T.za[:, 16:16 + C], 0.0, A.mult, A.add, chain=False)
+        bsa = scan(T.bs[:, C:2 * C], T.mu4[:], T.za[:, 0:C], 0.0, A.mult, A.add, chain=False, sig="c8")
+        tt(T.w22[:, 0:K], T.w2[:, 31:2 * C:32], T.w2[:, 2 * C + 31:4 * C:32], A.add)
+        bsm = tt(T.bsum[:, 0:88], T.bs[:, 3:C:4], T.bs[:, C + 3:2 * C:4], A.add, after=[bsa], chain=False, sig="c2")
+        ts(ow[:, 0:K:2], T.w22[:, 0:K // 2], 2.0 ** -16, A.mult, 256.0, A.min, sig="w")
+        w = ts(ow[:, 1:K:2], T.w22[:, K // 2:K], 2.0 ** -16, A.mult, 256.0, A.min, chain=False, sig="w")
         a_w = send(mate, lw[:], ow[:], "aw%d" % t, [w])
         a_q = send(mate, u8(lq[:]), u8(qX[:]), "aq%d" % t, [])
         if t == 0:
             for n in (1, 2):
                 tabs[n] = iota(T["tab%d" % n][:], [[0, 360]], 8, 0, "tb")
             tabs[1] = tabs[2]
-        scan(T.be[:], T.mb[:], T.bs[:, 3:384:4], 0.0, A.add, A.min, after=[("c8", t + 1)], chain=False)
+        scan(T.be[:], T.mb[:], T.bsum[:], 0.0, A.add, A.min, after=[bsm], chain=False)
         ts(T.bw[:, 0:6], T.be[:, 15:96:16], T.bcol[:, 0:1], A.add)
+        if t == 0:
+            ms(T.et[:, 512:1024], 0.0, chain=False, lane=1)
         for k in range(6):
-            ts(T.eq[:, 88 * k:88 * k + 88], T.bs[:, 3:C:4], T.bw[:, k:k + 1], A.not_equal, -128.0, A.mult, chain=k == 0)
+            ts(T.eq[:, 88 * k:88 * k + 88], T.bsum[:, 0:88], T.bw[:, k:k + 1], A.not_equal, -128.0, A.mult, chain=k == 0)
         scan(T.fs[:], T.dbl[:], T.eq[:], 0.0, A.add, A.max)
         tt(T.dup[:, 0:6], T.fs[:, 87:528:88], T.thm[:, 0:6], A.is_gt)
+        if t == 0:
+            ms(T.et[:, 1024:1536], 0.0, chain=False, lane=1)
         tt(T.dup[:, 0:6], T.dup[:, 0:6], T.dump[:, 0:6], A.mult)
+        if t == 0:
+            ms(T.et[:, 1536:2048], 0.0, chain=False, lane=1)
         tt(T.so[:, 0:6], T.dup[:, 0:6], T.bw[:, 0:6], A.max)
+        if t == 0:
+            ms(T.inc[:], 1.0, chain=False, lane=1)
         cp(T.soff[:, 0:6], T.so[:, 0:6])
         if t == 0:
-            ms(T.et[:, 1024:2048], 0.0, chain=False)
+            for b in range(4):
+                ts(T.et[:, 512 * b + b:512 * b + 512:4], T.idn[:], 0.0, A.is_equal, after=[i5], chain=b == 0, lane=1)
+            ms(T.inc[:, 0:C:4], -3.0, chain=False, lane=1)
         tb = cp(tab[:].indirect(T.soff[:, 0:6]), T.vals[:], after=[tabs[t]], sig="tab")
         if t == 0:
-            for b in range(4):
-                ts(T.et[:, 512 * b + b:512 * b + 512:4], T.idn[:], 0.0, A.is_equal, after=[i5], chain=False)
-            ms(T.inc[:], 1.0, chain=False)
             ms(T.ones[:], 1.0, chain=False)
             ms(T.px[:, 0:1], 4.0, chain=False)
             ms(T.d[:, 0:1], 0.0, chain=False)
@@ -245,57 +268,107 @@ def rank_program(g, core, T, topo):
             ms(T.ho[:, K:32], 0.0, chain=False)
             ts(T.pw2[:, 0:K], T.pw[:, 0:K], 2.0, A.mult, -float(C), A.add, chain=False)
             ts(T.hcol[:, 0:1], T.bcol[:, 0:1], 32760.0 / 1024.0, A.mult, 16384.0, A.add, chain=False)
-            ms(T.inc[:, 0:C:4], -3.0)
-            qe = quant(T.qe[:], T.se[:], T.et[:], chain=False, sig="qe")
+            qe = quant(T.qe[:], T.se[:], T.et[:], sig="qe", lane=1)
         if t == 1:
             qv = quant(T.qv[:], T.sv[:], T.vin[:], after=[ldv], chain=False, sig="qv")
-        val = act(T.val[:], tab[:].indirect(lw[:]), F.Relu, bias=2 * C * EPS, scale=-EPS / TINY, after=[tb, a_w],
-                  chain=False, sig="val")
-        tt(T.px[:, 1:C + 1], tab[:].indirect(lw[:]), T.alpha[:], A.min, after=[tb, a_w, i6], chain=t == 0)
-        scan(T.py[:], T.px[:, 0:C], T.px[:, 1:C + 1], 0.0, A.max, A.subtract)
-        ts(T.e1[:], T.py[:], 0.0, A.is_gt, 4.0, A.mult)
-        ts(T.e2[:], T.py[:], 4.0, A.min, chain=False)
-        pd = tt(T.pd[:], T.e1[:], T.e2[:], A.subtract, sig="pd")
-        phi = act(T.phi[:], T.pd[:], F.Identity, bias=12.0, scale=-4.0, after=[pd], chain=False, sig="phi")
-        ts(T.keep[:], T.pd[:], 1.5, A.is_lt, after=[pd], chain=False)
-        dn = scan(T.d[:, 1:C + 1], T.keep[:], T.pd[:], 0.0, A.mult, A.add, sig="d")
-        act(T.q[:], T.d[:, 0:C], F.Identity, bias=160.0 - 2.0 / 3.0, scale=1.0 / 3.0, after=[dn], chain=False)
-        q3 = act(T.q3[:], T.q[:], F.Identity, bias=480.0, scale=-3.0, sig="q3")
-        tt(T.pj[:], T.d[:, 0:C], T.phi[:], A.add, after=[dn, phi], chain=False)
-        pv = tt(T.pv[:], T.pj[:], T.q3[:], A.add, after=[q3], sig="pv")
-        v2 = act(T.v2[:], T.pv[:], F.Identity, bias=2.0, after=[pv], chain=False, sig="v2")
-        ts(T.e1[:], T.pv[:], GRID, A.add, GRID + 8.0, A.is_equal, after=[pv], chain=False)
-        ts(T.e2[:], T.pv[:], GRID, A.add, GRID + 4.0, A.is_equal, chain=False)
-        ts(T.pa[:], T.e1[:], -2.0, A.mult, 1.0, A.add)
-        ts(T.rst[:], T.e2[:], 5.0, A.mult, -2.5, A.add, chain=False)
-        scan(T.gm[:, 1:C + 1], T.pa[:], T.rst[:], 2.5, A.mult, A.max)
-        tt(T.pz[:], T.v2[:], T.gm[:, 0:C], A.add, after=[v2])
-        ts(T.nl[:, 1:C + 1], T.pz[:], GRID, A.add, GRID + 8.0, A.not_equal)
-        scan(T.st[:], T.inc[:], T.nl[:, 0:C], 0.0, A.add, A.mult)
-        cn = scan(T.cnt[:], T.ones[:], T.nl[:, 1:C + 1], 0.0, A.add, A.subtract, chain=False, sig="cnt")
-        for b in range(4):
-            dm = mm(T.psr[:, 512 * b:512 * b + C], T.qe[:, 128 * b:128 * b + 128], T.se[:, 128 * b:128 * b + 128],
-                    lq[:], ls[:], after=[qe, a_s, a_q], sig="dm%d" % b)
-            dcp = act(pl[:, PL * b + C:PL * b + 2 * C], T.psr[:, 512 * b:512 * b + C], F.Identity, scale=64.0,
-                      after=[dm], chain=False, sig="dcp")
-        acc = act(T.sgn[:], T.cnt[:], F.Sign, bias=128.5, scale=-1.0, acc=T.acc[:, 0:1], after=[cn], chain=False,
-                  sig="acc")
-        ts(T.d0[:], T.st[:], 0.0, A.is_equal, -4096.0 * EPS, A.add)
-        scan(T.hh[:], T.d0[:], T.val[:], 0.0, A.add, A.min, after=[val])
-        scan(T.he[:], T.m16[:], T.hh[:], 0.0, A.add, A.min, after=[cm16])
-        ts(T.hu[:, 0:K], T.pw2[:, 0:K], T.acc[:, 0:1], A.is_lt, float(C), A.mult, after=[acc], chain=False)
-        ts(T.hi[:, 0:K], T.he[:, 15:C:16], 4095.0 / 4096.0 / EPS, A.mult, T.hcol[:, 0:1], A.add)
-        tt(T.h1[:, 0:K], T.hu[:, 0:K], T.pw[:, 0:K], A.add, chain=False)
-        ts(T.hj[:, 0:K], T.hi[:, 0:K], 4095, A.bitwise_and)
-        tt(T.hf[:, 0:K], T.hj[:, 0:K], T.h1[:, 0:K], A.max)
-        off = cp(T.off[:, 0:K], T.hf[:, 0:K], sig="off")
-        pre = [off, dcp, plane]
-        for b in (0, 1):
-            gv = ts(T.gt[:, b:4 * C:4], pl[:, PL * b:PL * b + PL].indirect(T.off[:, 0:K]), 0.015625, A.mult,
-                    after=pre, chain=False, sig="gv")
-        for b in (2, 3):
-            gs = act(T.gt[:, b:4 * C:4], pl[:, PL * b:PL * b + PL].indirect(T.off[:, 0:K]), F.Identity, scale=0.015625,
-                     after=pre, chain=False, sig="gs")
+
+        tok = {}
+
+        def step(s, h):
+            a, b = HALF[h]
+            ka, kb = a // 16, b // 16
+            n = str(h)
+
+            def init(buf, at, first):
+                return buf[:, at:at + 1] if h else first
+
+            if s == 0:
+                tok["val", h] = act(T.val[:, a:b], tab[:].indirect(lw[:, ka:kb]), F.Relu, bias=2 * C * EPS,
+                                    scale=-EPS / TINY, after=[tb, a_w], chain=False, sig="val" + n)
+                tt(T.px[:, a + 1:b + 1], tab[:].indirect(lw[:, ka:kb]), T.alpha[:, a:b], A.min, after=[tb, a_w, i6], lane=h)
+            elif s == 1:
+                scan(T.py[:, a:b], T.px[:, a:b], T.px[:, a + 1:b + 1], init(T.py, a - 1, 0.0), A.max, A.subtract, lane=h)
+            elif s == 2:
+                ts(T.e1[:, a:b], T.py[:, a:b], 0.0, A.is_gt, 4.0, A.mult, lane=h)
+                ts(T.e2[:, a:b], T.py[:, a:b], 4.0, A.min, chain=False, lane=h)
+            elif s == 3:
+                pd = tok["pd", h] = tt(T.pd[:, a:b], T.e1[:, a:b], T.e2[:, a:b], A.subtract, sig="pd" + n, lane=h)
+                tok["phi", h] = act(T.phi[:, a:b], T.pd[:, a:b], F.Identity, bias=12.0, scale=-4.0, after=[pd],
+                                    chain=False, sig="phi" + n)
+            elif s == 4:
+                ts(T.keep[:, a:b], T.pd[:, a:b], 1.5, A.is_lt, after=[tok["pd", h]], chain=False, lane=h)
+            elif s == 5:
+                dn = tok["d", h] = scan(T.d[:, a + 1:b + 1], T.keep[:, a:b], T.pd[:, a:b], init(T.d, a, 0.0),
+                                        A.mult, A.add, sig="d" + n, lane=h)
+                act(T.q[:, a:b], T.d[:, a:b], F.Identity, bias=160.0 - 2.0 / 3.0, scale=1.0 / 3.0, after=[dn],
+                    chain=False, lane=h)
+            elif s == 6:
+                tok["q3", h] = act(T.q3[:, a:b], T.q[:, a:b], F.Identity, bias=480.0, scale=-3.0, sig="qq" + n, lane=h)
+                tt(T.pj[:, a:b], T.d[:, a:b], T.phi[:, a:b], A.add, after=[tok["d", h], tok["phi", h]], chain=False, lane=h)
+            elif s == 7:
+                pv = tok["pv", h] = tt(T.pv[:, a:b], T.pj[:, a:b], T.q3[:, a:b], A.add, after=[tok["q3", h]],
+                                       sig="pv" + n, lane=h)
+                tok["v2", h] = act(T.v2[:, a:b], T.pv[:, a:b], F.Identity, bias=2.0, after=[pv], chain=False, sig="vv" + n)
+                if h:
+                    for j in range(4):
+                        dm = mm(T.psr[:, 512 * j:512 * j + C], T.qe[:, 128 * j:128 * j + 128],
+                                T.se[:, 128 * j:128 * j + 128], lq[:], ls[:], after=[qe, a_s, a_q], sig="dm%d" % j)
+                        tok["dcp"] = act(pl[:, PL * j + C:PL * j + 2 * C], T.psr[:, 512 * j:512 * j + C], F.Identity,
+                                         scale=64.0, after=[dm], chain=False, sig="dcp")
+            elif s == 8:
+                ts(T.e1[:, a:b], T.pv[:, a:b], GRID, A.add, GRID + 8.0, A.is_equal, after=[tok["pv", h]], chain=False, lane=h)
+                ts(T.e2[:, a:b], T.pv[:, a:b], GRID, A.add, GRID + 4.0, A.is_equal, chain=False, lane=h)
+            elif s == 9:
+                ts(T.pa[:, a:b], T.e1[:, a:b], -2.0, A.mult, 1.0, A.add, lane=h)
+                ts(T.rst[:, a:b], T.e2[:, a:b], 5.0, A.mult, -2.5, A.add, chain=False, lane=h)
+            elif s == 10:
+                scan(T.gm[:, a + 1:b + 1], T.pa[:, a:b], T.rst[:, a:b], init(T.gm, a, 2.5), A.mult, A.max, lane=h)
+            elif s == 11:
+                tt(T.pz[:, a:b], T.v2[:, a:b], T.gm[:, a:b], A.add, after=[tok["v2", h]], lane=h)
+            elif s == 12:
+                ts(T.nl[:, a + 1:b + 1], T.pz[:, a:b], GRID, A.add, GRID + 8.0, A.not_equal, lane=h)
+            elif s == 13:
+                scan(T.st[:, a:b], T.inc[:, a:b], T.nl[:, a:b], init(T.st, a - 1, 0.0), A.add, A.mult, lane=h)
+                tok["cnt", h] = scan(T.cnt[:, a:b], T.ones[:, a:b], T.nl[:, a + 1:b + 1], init(T.cnt, a - 1, 0.0), A.add,
+                                     A.subtract, after=[tok["cnt", 0]] if h else [], chain=False, sig="cnt" + n)
+                if h:
+                    tok["acc"] = act(T.sgn[:], T.cnt[:], F.Sign, bias=128.5, scale=-1.0, acc=T.acc[:, 0:1],
+                                     after=[tok["cnt", 0], tok["cnt", 1]], chain=False, sig="acc")
+            elif s == 14:
+                ts(T.d0[:, a:b], T.st[:, a:b], 0.0, A.is_equal, -4096.0 * EPS, A.add, lane=h)
+            elif s == 15:
+                scan(T.hh[:, a:b], T.d0[:, a:b], T.val[:, a:b], init(T.hh, a - 1, 0.0), A.add, A.min,
+                     after=[tok["val", h]], lane=h)
+            elif s == 16:
+                scan(T.he[:, a:b], T.m16[:, a:b], T.hh[:, a:b], 0.0, A.add, A.min, after=[cm16], lane=h)
+            elif s == 17:
+                ts(T.hi[:, ka:kb], T.he[:, a + 15:b:16], 4095.0 / 4096.0 / EPS, A.mult, T.hcol[:, 0:1], A.add, lane=h)
+                if not h:
+                    tok["hu"] = ts(T.hu[:, 0:K], T.pw2[:, 0:K], T.acc[:, 0:1], A.is_lt, float(C), A.mult,
+                                   after=[tok["acc"]], chain=False, sig="hu")
+            elif s == 18:
+                ts(T.hj[:, ka:kb], T.hi[:, ka:kb], 4095, A.bitwise_and, lane=h)
+                if not h:
+                    tok["h1"] = tt(T.h1[:, 0:K], T.hu[:, 0:K], T.pw[:, 0:K], A.add, after=[tok["hu"]], chain=False, sig="h1")
+            elif s == 19:
+                tt(T.hf[:, ka:kb], T.hj[:, ka:kb], T.h1[:, ka:kb], A.max, after=[tok["h1"]], lane=h)
+            elif s == 20:
+                tok["off", h] = cp(T.off[:, ka:kb], T.hf[:, ka:kb], sig="off" + n, lane=h)
+            else:
+                pre = [tok["off", h], tok["dcp"], plane]
+                for j in (0, 1):
+                    tok["gv"] = ts(T.gt[:, 4 * a + j:4 * b:4], pl[:, PL * j:PL * j + PL].indirect(T.off[:, ka:kb]),
+                                   0.015625, A.mult, after=pre, chain=False, sig="gv")
+                for j in (2, 3):
+                    tok["gs"] = act(T.gt[:, 4 * a + j:4 * b:4], pl[:, PL * j:PL * j + PL].indirect(T.off[:, ka:kb]),
+                                    F.Identity, scale=0.015625, after=pre, chain=False, sig="gs")
+
+        step(0, 0)
+        for s in range(21):
+            step(s + 1, 0)
+            step(s, 1)
+        step(21, 1)
+        gv, gs = tok["gv"], tok["gs"]
         if t == 2:
             ts(T.hu[:, 0:K], T.hf[:, 0:K], 2.0 * C - 0.5, A.is_gt, -2.0 * C, A.mult, chain=False)
         qg = quant(T.qg[:], T.sg[:], T.gt[:], after=[gv, gs], chain=False, sig="qg")
@@ -323,10 +396,6 @@ def rank_program(g, core, T, topo):
                      chain=False, sig="xs")
         ts(T.xt[:, 3:4 * C:4], pn[:, PL * 3 + 2 * C:PL * 4], 0.015625, A.mult, after=[ys[3]], chain=False)
         qx = quant(T["qx%d" % (t + 1)][:], T["sx%d" % (t + 1)][:], T.xt[:], after=[xs], sig="qx")
-        if t < 2:
-            for b in range(4):
-                plane = act(pn[:, PL * b:PL * b + C], pn[:, PL * b + 2 * C:PL * b + PL], F.Copy, after=[ys[b]],
-                            chain=False, sig="pl")
 
     ym = mm(T.psa[:, 0:C], T.qv[:], T.sv[:], T.qx3[:], T.sx3[:], after=[qx, qv], sig="ym")
     dma("Y", T.oc[:], u8(T.qx3[:]), "stc", after=[qx])

from concourse.mybir import dt, AluOpType as A, ActivationFunctionType as F

C = 352
K = C // 16
PL = 3 * C
HALF = ((0, 160), (160, C))
Q4, U8, BF, F32, I32, U16 = "float8_e4m3fn_x4", "uint8", "bfloat16", "float32", "int32", "uint16"


def _sb(n, d):
    return ("sbuf", [128, n], d)


SCRATCH = {
    "xin": _sb(4 * C, BF), "uin": _sb(512, BF), "vin": _sb(512, BF),
    "qu": _sb(128, Q4), "su": _sb(128, U8), "qup": _sb(256, Q4), "sup": _sb(256, U8),
    "qv": _sb(128, Q4), "sv": _sb(128, U8), "qw": _sb(512, Q4), "sw": _sb(512, U8),
    "et": _sb(2048, BF), "qe": _sb(512, Q4), "se": _sb(512, U8),
    "gt": _sb(4 * C, BF), "g64": _sb(4 * C, BF), "xt": _sb(4 * C, BF), "qg": _sb(C, Q4), "sg": _sb(C, U8),
    "yb": _sb(C, F32),
    "pcol": _sb(4, I32), "rint": _sb(4, I32), "rcol": _sb(4, F32), "bcol": _sb(4, F32), "j32": _sb(32, F32),
    "t32": _sb(32, F32), "ca": _sb(32, F32), "cb": _sb(32, F32), "cc": _sb(32, F32), "cd": _sb(32, F32),
    "ce": _sb(32, F32), "cf": _sb(16, F32), "cg": _sb(16, F32), "hcol": _sb(4, F32),
    "ui": _sb(16, I32), "uoff": _sb(16, U16), "k16": _sb(24, F32), "pw": _sb(24, F32), "pw2": _sb(24, F32),
    "th0": _sb(16, F32), "thm": _sb(8, F32), "dump": _sb(8, F32), "idn": _sb(128, F32),
    "vi": _sb(96, F32), "vals": _sb(96, F32), "alpha": _sb(C, BF), "mu32": _sb(C, BF), "mu4": _sb(C, BF),
    "m16": _sb(C, BF), "mb": _sb(96, BF), "dbl": _sb(528, BF), "ones": _sb(C, BF), "inc": _sb(C, BF),
    "za": _sb(368, BF), "zb": _sb(368, BF), "w2": _sb(4 * C, BF), "w22": _sb(24, F32), "bs": _sb(2 * C, BF),
    "bsum": _sb(96, BF), "be": _sb(96, F32), "bw": _sb(8, F32), "eq": _sb(528, BF), "fs": _sb(528, BF),
    "dup": _sb(8, F32), "so": _sb(8, F32), "soff": _sb(8, U16),
    "px": _sb(368, BF), "py": _sb(C, BF), "pd": _sb(C, BF), "keep": _sb(C, BF),
    "d": _sb(368, BF), "q": _sb(C, BF), "q3": _sb(C, BF), "pj": _sb(C, BF), "phi": _sb(C, BF), "pv": _sb(C, BF),
    "v2": _sb(C, BF), "e1": _sb(C, BF), "e2": _sb(C, BF), "pa": _sb(C, BF), "rst": _sb(C, BF), "gm": _sb(368, BF),
    "pz": _sb(C, BF), "nl": _sb(368, BF), "cnt": _sb(C, BF), "sgn": _sb(C, BF), "acc": _sb(4, F32),
    "st": _sb(C, BF), "d0": _sb(C, BF), "val": _sb(C, F32), "hh": _sb(C, F32),
    "he": _sb(C, F32), "hi": _sb(24, I32), "hj": _sb(24, I32), "h1": _sb(24, F32), "hu": _sb(24, F32),
    "hf": _sb(24, F32), "ho": _sb(32, F32), "ht": _sb(32, F32), "off": _sb(24, U16),
    "psa": ("psum", [128, 1024], F32), "psr": ("psum", [128, 2048], F32),
}
for _t in range(4):
    SCRATCH["qx%d" % _t] = _sb(C, Q4)
    SCRATCH["sx%d" % _t] = _sb(C, U8)
for _t in range(3):
    SCRATCH["lq%d" % _t] = _sb(C, Q4)
    SCRATCH["ls%d" % _t] = _sb(C, U8)
    SCRATCH["lw%d" % _t] = _sb(K, U16)
    SCRATCH["ow%d" % _t] = _sb(K, U16)
    SCRATCH["pl%d" % _t] = _sb(4 * PL, BF)
    SCRATCH["tab%d" % _t] = _sb(360, F32)

SEMAPHORES = (["V", "S", "T", "G", "V1", "S1", "ldx", "ldu", "ldw", "ldv", "stc", "sty", "sto", "sent",
               "i0", "i1", "i2", "i3", "i4", "i5", "i6", "tb", "c0", "c1", "c2", "c3", "c4", "c5", "c6", "c7", "c8",
               "qx", "sa", "sb", "w", "tab", "acc", "gv", "gs", "qg", "za", "hu", "h1",
               "xs", "dcp", "qe", "qv", "ym", "yc", "ht", "pl", "tb0"]
              + ["%s%d" % (n, h) for n in ("val", "pd", "phi", "pv", "vv", "cnt", "off", "d", "qq") for h in range(2)]
              + ["%s%d" % (n, b) for n in ("r", "dm", "gb", "ya") for b in range(4)]
              + ["%s%d" % (n, t) for n in ("as", "aw", "aq") for t in range(3)])

EPS = 2.0 ** -15
TINY = 2.0 ** -40
GRID = 2.0 ** 25


def rank_program(g, core, T, topo):
    rank = T.rank_of(core)
    if rank is None:
        return
    queue = {"V": g.vector, "S": g.scalar, "T": g.tensor, "G": g, "Y": g.sync}
    cnt, seen = {}, {e: {} for e in queue}

    def wait(e, tok):
        name, n = tok
        if seen[e].get(name, 0) < n:
            queue[e].wait_ge(T.sem[name], n)
            seen[e][name] = n

    def op(e, call, after=(), chain=True, sig=None, inc=1, lane=0):
        own = e + ("1" if lane else "")
        if chain and cnt.get(own, 0):
            wait(e, (own, cnt[own]))
        for tok in after:
            wait(e, tok)
        name = sig or own
        call().then_inc(T.sem[name], inc)
        cnt[name] = cnt.get(name, 0) + inc
        return (name, cnt[name])

    V, S = g.vector, g.scalar

    def ts(out, in0, s1, o0, s2=None, o1=None, **k):
        if o1 is None:
            return op("V", lambda: V.tensor_scalar(out, in0, s1, None, o0), **k)
        return op("V", lambda: V.tensor_scalar(out, in0, s1, s2, o0, o1), **k)

    def tt(out, a, b, o, **k):
        return op("V", lambda: V.tensor_tensor(out, a, b, o), **k)

    def cp(out, a, **k):
        return op("V", lambda: V.tensor_copy(out, a), **k)

    def ms(out, c, **k):
        return op("V", lambda: V.memset(out, c), **k)

    def scan(out, a, b, init, o0, o1, **k):
        return op("V", lambda: V.tensor_tensor_scan(out, a, b, init, o0, o1), **k)

    def act(out, a, f, bias=0.0, scale=1.0, acc=None, **k):
        if f == F.Copy and scale == 1.0:
            return op("S", lambda: S.activation(out, a, f), **k)
        if acc is not None:
            return op("S", lambda: S.activation(out, a, f, bias=bias, scale=scale, accum_out=acc), **k)
        return op("S", lambda: S.activation(out, a, f, bias=bias, scale=scale), **k)

    def mm(out, lq, ls, rq, rs, **k):
        return op("T", lambda: g.tensor.matmul_mx(out, lq, ls, rq, rs, True, True), chain=False, **k)

    def quant(q, s, x, **k):
        return op("V", lambda: V.quantize_mx(q, s, x), **k)

    def iota(out, pat, base, cm, sig, fl=True):
        if fl:
            return op("G", lambda: g.iota(out, pat, base, cm, allow_small_or_imprecise_dtypes=True), chain=False, sig=sig)
        return op("G", lambda: g.iota(out, pat, base, cm), chain=False, sig=sig)

    def dma(e, out, a, sig, after=()):
        return op(e, lambda: queue[e].dma_start(out, a), after=after, chain=False, sig=sig, inc=16)

    def send(dst, out, a, sem, after):
        for tok in after:
            wait("G", tok)
        rid, pid = topo.addr(dst, core)
        n = len(topo.engines(core, dst))
        g.remote_dma(out, a, T.sem[sem], T.sem["sent"], pid, rid, topo.mask(core, dst))
        cnt["sent"] = cnt.get("sent", 0) + n
        cnt[sem] = len(topo.engines(dst, core))
        return (sem, cnt[sem])

    def u8(v):
        return v.bitcast(dt.uint8)

    ldu = dma("S", T.uin[:], T.u[:], "ldu")
    ldx = dma("Y", T.xin[:], T.x[:], "ldx")
    dma("Y", u8(T.qw[:]), T.wc[:], "ldw", after=[ldx])
    ldw = dma("Y", T.sw[:], T.ws[:], "ldw")
    ldv = dma("Y", T.vin[:], T.v[:], "ldv")

    i0 = iota(T.pcol[:, 0:1], [[0, 1]], 0, 1, "i0", False)
    i1 = iota(T.j32[:], [[1, 32]], 0, 0, "i1")
    i2 = iota(T.ui[:], [[1, 2], [16, 8]], 0, 0, "i2", False)
    i3 = iota(T.k16[:, 0:K], [[16, K]], 0, 0, "i3")
    i4 = iota(T.vi[:], [[-4, 96]], 0, 0, "i4")
    i5 = iota(T.idn[:], [[-1, 128]], 0, 1, "i5")
    i6 = iota(T.alpha[:], [[0, C // 4], [-1, 4]], 7, 0, "i6")
    tabs = {0: iota(T.tab0[:], [[0, 360]], 8, 0, "tb0")}

    ms(T.mu4[:], 4.0)
    ms(T.za[:, C:368], 0.0, chain=False)
    ms(T.zb[:, C:368], 0.0, chain=False)
    ts(T.rint[:, 0:1], T.pcol[:, 0:1], 15, A.bitwise_and, after=[i0], chain=False)
    cp(T.rcol[:, 0:1], T.rint[:, 0:1])
    ms(T.mu4[:, 0:C:4], 0.0, chain=False)
    ms(T.zb[:, C:C + 3], 256.0, chain=False)
    uoff = cp(T.uoff[:], T.ui[:], after=[i2], chain=False, sig="c0")
    ts(T.t32[:], T.j32[:], T.rcol[:, 0:1], A.subtract, after=[i1])
    ts(T.pw[:, 0:K], T.k16[:, 0:K], T.rcol[:, 0:1], A.add, after=[i3], chain=False)
    ts(T.bcol[:, 0:1], T.rcol[:, 0:1], 14.5, A.is_lt, 1024.0, A.mult, chain=False)
    ts(T.ca[:], T.t32[:], 4.0, A.is_equal, 65532.0, A.mult)
    ts(T.cb[:], T.t32[:], 0.0, A.is_equal, -4.0, A.mult, chain=False)
    ts(T.cc[:], T.t32[:], 4.0, A.is_le, 3.0, A.mult, chain=False)
    ts(T.cf[:], T.t32[:, 0:16], 1.0, A.is_equal, chain=False)
    tt(T.cd[:], T.ca[:], T.cb[:], A.add)
    tt(T.cg[:], T.cb[:, 0:16], T.cf[:], A.add, chain=False)
    ts(T.th0[:, 0:6], T.pw[:, 0:6], -1.0, A.mult, 87.0, A.add, chain=False)
    ts(T.th0[:, 8:14], T.pw[:, 0:6], 87.5, A.is_gt, -1000.0, A.mult, chain=False)
    c1 = tt(T.ce[:], T.cd[:], T.cc[:], A.add, sig="c1")
    tt(T.thm[:, 0:6], T.th0[:, 0:6], T.th0[:, 8:14], A.add, chain=False)
    ms(T.bsum[:, 88:96], 0.0, chain=False)
    ms(T.dbl[:], 1.0, chain=False)
    ts(T.dump[:, 0:6], T.pw[:, 0:6], 257.0, A.add, chain=False)
    ts(T.vals[:], T.vi[:], TINY, A.mult, after=[i4], chain=False)
    act(T.mu32[:, 0:32], T.ce[:], F.Identity, bias=1.0, after=[c1])
    act(T.m16[:, 0:16], T.cg[:], F.Identity, scale=-1.0, chain=False)
    act(T.mu32[:, 32:64], T.mu32[:, 0:32], F.Copy)
    act(T.m16[:, 16:32], T.m16[:, 0:16], F.Copy, chain=False)
    act(T.mu32[:, 64:128], T.mu32[:, 0:64], F.Copy)
    act(T.m16[:, 32:64], T.m16[:, 0:32], F.Copy, chain=False)

    qu = quant(T.qu[:], T.su[:], T.uin[:], after=[ldu], chain=False, sig="c4")
    pq = cp(T.qup[:].bitcast(dt.uint32), T.qu[:].bitcast(dt.uint32).indirect(T.uoff[:]), after=[qu, uoff],
            chain=False, sig="c5")
    ps = act(T.sup[:], T.su[:].indirect(T.uoff[:]), F.Copy, after=[qu, uoff], chain=False, sig="c6")
    act(T.mu32[:, 128:256], T.mu32[:, 0:128], F.Copy)
    act(T.mu32[:, 256:C], T.mu32[:, 0:96], F.Copy, chain=False)
    act(T.m16[:, 64:128], T.m16[:, 0:64], F.Copy, chain=False)
    cmb = act(T.mb[:], T.m16[:, 0:96], F.Identity, scale=1024.0, sig="c3")
    act(T.m16[:, 128:256], T.m16[:, 0:128], F.Copy, chain=False, sig="c7")
    cm16 = act(T.m16[:, 256:C], T.m16[:, 0:96], F.Copy, chain=False, sig="c7")
    qx = quant(T.qx0[:], T.sx0[:], T.xin[:], after=[ldx], chain=False, sig="qx")
    ms(T.dbl[:, 0:528:88], -1024.0)
    ms(T.et[:, 0:512], 0.0, chain=False)

    w = cmb
    ys = []
    for t in range(3):
        mate = T.cores[rank ^ (1 << t)]
        qX, sX, lq, ls = T["qx%d" % t], T["sx%d" % t], T["lq%d" % t], T["ls%d" % t]
        lw, ow, pl, pn, tab = T["lw%d" % t], T["ow%d" % t], T["pl%d" % t], T["pl%d" % ((t + 1) % 3)], T["tab%d" % t]
        a_s = send(mate, ls[:], sX[:], "as%d" % t, [qx])
        sb = mm(T.psa[:, 512:512 + C], T.qup[:, 128:256], T.sup[:, 128:256], qX[:], sX[:], after=[qx, pq, ps], sig="sb")
        sa = mm(T.psa[:, 0:C], T.qup[:, 0:128], T.sup[:, 0:128], qX[:], sX[:], sig="sa")
        for h, (a, b) in enumerate(HALF):
            act(T.sgn[:, a:b], T.psa[:, a:b], F.Sign, after=[sa], chain=False, lane=h)
        for h, (a, b) in enumerate(HALF):
            za = act(T.za[:, a:b], T.sgn[:, a:b], F.Relu, scale=2.0, lane=h, sig="za")
        for b in range(4):
            if t == 0:
                for at in (0, 2 * C):
                    plane = act(pl[:, PL * b + at:PL * b + at + C], T.xin[:, b:4 * C:4], F.Identity, scale=64.0,
                                after=[ldx], chain=False, sig="pl")
            else:
                plane = act(pl[:, PL * b:PL * b + C], pl[:, PL * b + 2 * C:PL * b + PL], F.Copy, after=[ys[b]],
                            chain=False, sig="pl")
        ts(T.zb[:, 0:C], T.psa[:, 512:512 + C], 0.0, A.is_gt, after=[sb], chain=False)
        scan(T.w2[:, 0:C], T.mu32[:], T.zb[:, 0:C], 0.0, A.mult, A.add, after=[w])
        scan(T.w2[:, C:2 * C], T.mu32[:], T.zb[:, 16:16 + C], 0.0, A.mult, A.add, chain=False)
        scan(T.bs[:, 0:C], T.mu4[:], T.zb[:, 0:C], 0.0, A.mult, A.add, chain=False)
        scan(T.w2[:, 2 * C:3 * C], T.mu32[:], T.za[:, 0:C], 0.0, A.mult, A.add, after=[za], chain=False)
        scan(T.w2[:, 3 * C:4 * C], T.mu32[:], T.za[:, 16:16 + C], 0.0, A.mult, A.add, chain=False)
        bsa = scan(T.bs[:, C:2 * C], T.mu4[:], T.za[:, 0:C], 0.0, A.mult, A.add, chain=False, sig="c8")
        tt(T.w22[:, 0:K], T.w2[:, 31:2 * C:32], T.w2[:, 2 * C + 31:4 * C:32], A.add)
        bsm = tt(T.bsum[:, 0:88], T.bs[:, 3:C:4], T.bs[:, C + 3:2 * C:4], A.add, after=[bsa], chain=False, sig="c2")
        ts(ow[:, 0:K:2], T.w22[:, 0:K // 2], 2.0 ** -16, A.mult, 256.0, A.min, sig="w")
        w = ts(ow[:, 1:K:2], T.w22[:, K // 2:K], 2.0 ** -16, A.mult, 256.0, A.min, chain=False, sig="w")
        a_w = send(mate, lw[:], ow[:], "aw%d" % t, [w])
        a_q = send(mate, u8(lq[:]), u8(qX[:]), "aq%d" % t, [])
        if t == 0:
            for n in (1, 2):
                tabs[n] = iota(T["tab%d" % n][:], [[0, 360]], 8, 0, "tb")
            tabs[1] = tabs[2]
        scan(T.be[:], T.mb[:], T.bsum[:], 0.0, A.add, A.min, after=[bsm], chain=False)
        ts(T.bw[:, 0:6], T.be[:, 15:96:16], T.bcol[:, 0:1], A.add)
        if t == 0:
            ms(T.et[:, 512:1024], 0.0, chain=False, lane=1)
        for k in range(6):
            ts(T.eq[:, 88 * k:88 * k + 88], T.bsum[:, 0:88], T.bw[:, k:k + 1], A.not_equal, -128.0, A.mult, chain=k == 0)
        scan(T.fs[:], T.dbl[:], T.eq[:], 0.0, A.add, A.max)
        tt(T.dup[:, 0:6], T.fs[:, 87:528:88], T.thm[:, 0:6], A.is_gt)
        if t == 0:
            ms(T.et[:, 1024:1536], 0.0, chain=False, lane=1)
        tt(T.dup[:, 0:6], T.dup[:, 0:6], T.dump[:, 0:6], A.mult)
        if t == 0:
            ms(T.et[:, 1536:2048], 0.0, chain=False, lane=1)
        tt(T.so[:, 0:6], T.dup[:, 0:6], T.bw[:, 0:6], A.max)
        if t == 0:
            ms(T.inc[:], 1.0, chain=False, lane=1)
        cp(T.soff[:, 0:6], T.so[:, 0:6])
        if t == 0:
            for b in range(4):
                ts(T.et[:, 512 * b + b:512 * b + 512:4], T.idn[:], 0.0, A.is_equal, after=[i5], chain=b == 0, lane=1)
            ms(T.inc[:, 0:C:4], -3.0, chain=False, lane=1)
        tb = cp(tab[:].indirect(T.soff[:, 0:6]), T.vals[:], after=[tabs[t]], sig="tab")
        if t == 0:
            ms(T.ones[:], 1.0, chain=False)
            ms(T.px[:, 0:1], 4.0, chain=False)
            ms(T.d[:, 0:1], 0.0, chain=False)
            ms(T.gm[:, 0:1], 2.5, chain=False)
            ms(T.nl[:, 0:1], 0.0, chain=False)
            ms(T.ho[:, K:32], 0.0, chain=False)
            ts(T.pw2[:, 0:K], T.pw[:, 0:K], 2.0, A.mult, -float(C), A.add, chain=False)
            ts(T.hcol[:, 0:1], T.bcol[:, 0:1], 32760.0 / 1024.0, A.mult, 16384.0, A.add, chain=False)
            qe = quant(T.qe[:], T.se[:], T.et[:], sig="qe", lane=1)
        if t == 1:
            qv = quant(T.qv[:], T.sv[:], T.vin[:], after=[ldv], chain=False, sig="qv")

        tok = {}

        def step(s, h):
            a, b = HALF[h]
            ka, kb = a // 16, b // 16
            n = str(h)

            def init(buf, at, first):
                return buf[:, at:at + 1] if h else first

            if s == 0:
                tok["val", h] = act(T.val[:, a:b], tab[:].indirect(lw[:, ka:kb]), F.Relu, bias=2 * C * EPS,
                                    scale=-EPS / TINY, after=[tb, a_w], chain=False, sig="val" + n)
                tt(T.px[:, a + 1:b + 1], tab[:].indirect(lw[:, ka:kb]), T.alpha[:, a:b], A.min, after=[tb, a_w, i6], lane=h)
            elif s == 1:
                scan(T.py[:, a:b], T.px[:, a:b], T.px[:, a + 1:b + 1], init(T.py, a - 1, 0.0), A.max, A.subtract, lane=h)
            elif s == 2:
                ts(T.e1[:, a:b], T.py[:, a:b], 0.0, A.is_gt, 4.0, A.mult, lane=h)
                ts(T.e2[:, a:b], T.py[:, a:b], 4.0, A.min, chain=False, lane=h)
            elif s == 3:
                pd = tok["pd", h] = tt(T.pd[:, a:b], T.e1[:, a:b], T.e2[:, a:b], A.subtract, sig="pd" + n, lane=h)
                tok["phi", h] = act(T.phi[:, a:b], T.pd[:, a:b], F.Identity, bias=12.0, scale=-4.0, after=[pd],
                                    chain=False, sig="phi" + n)
            elif s == 4:
                ts(T.keep[:, a:b], T.pd[:, a:b], 1.5, A.is_lt, after=[tok["pd", h]], chain=False, lane=h)
            elif s == 5:
                dn = tok["d", h] = scan(T.d[:, a + 1:b + 1], T.keep[:, a:b], T.pd[:, a:b], init(T.d, a, 0.0),
                                        A.mult, A.add, sig="d" + n, lane=h)
                act(T.q[:, a:b], T.d[:, a:b], F.Identity, bias=160.0 - 2.0 / 3.0, scale=1.0 / 3.0, after=[dn],
                    chain=False, lane=h)
            elif s == 6:
                tok["q3", h] = act(T.q3[:, a:b], T.q[:, a:b], F.Identity, bias=480.0, scale=-3.0, sig="qq" + n, lane=h)
                tt(T.pj[:, a:b], T.d[:, a:b], T.phi[:, a:b], A.add, after=[tok["d", h], tok["phi", h]], chain=False, lane=h)
            elif s == 7:
                pv = tok["pv", h] = tt(T.pv[:, a:b], T.pj[:, a:b], T.q3[:, a:b], A.add, after=[tok["q3", h]],
                                       sig="pv" + n, lane=h)
                tok["v2", h] = act(T.v2[:, a:b], T.pv[:, a:b], F.Identity, bias=2.0, after=[pv], chain=False, sig="vv" + n)
                if h:
                    for j in range(4):
                        dm = mm(T.psr[:, 512 * j:512 * j + C], T.qe[:, 128 * j:128 * j + 128],
                                T.se[:, 128 * j:128 * j + 128], lq[:], ls[:], after=[qe, a_s, a_q], sig="dm%d" % j)
                        tok["dcp"] = act(pl[:, PL * j + C:PL * j + 2 * C], T.psr[:, 512 * j:512 * j + C], F.Identity,
                                         scale=64.0, after=[dm], chain=False, sig="dcp")
            elif s == 8:
                ts(T.e1[:, a:b], T.pv[:, a:b], GRID, A.add, GRID + 8.0, A.is_equal, after=[tok["pv", h]], chain=False, lane=h)
                ts(T.e2[:, a:b], T.pv[:, a:b], GRID, A.add, GRID + 4.0, A.is_equal, chain=False, lane=h)
            elif s == 9:
                ts(T.pa[:, a:b], T.e1[:, a:b], -2.0, A.mult, 1.0, A.add, lane=h)
                ts(T.rst[:, a:b], T.e2[:, a:b], 5.0, A.mult, -2.5, A.add, chain=False, lane=h)
            elif s == 10:
                scan(T.gm[:, a + 1:b + 1], T.pa[:, a:b], T.rst[:, a:b], init(T.gm, a, 2.5), A.mult, A.max, lane=h)
            elif s == 11:
                tt(T.pz[:, a:b], T.v2[:, a:b], T.gm[:, a:b], A.add, after=[tok["v2", h]], lane=h)
            elif s == 12:
                ts(T.nl[:, a + 1:b + 1], T.pz[:, a:b], GRID, A.add, GRID + 8.0, A.not_equal, lane=h)
            elif s == 13:
                scan(T.st[:, a:b], T.inc[:, a:b], T.nl[:, a:b], init(T.st, a - 1, 0.0), A.add, A.mult, lane=h)
                tok["cnt", h] = scan(T.cnt[:, a:b], T.ones[:, a:b], T.nl[:, a + 1:b + 1], init(T.cnt, a - 1, 0.0), A.add,
                                     A.subtract, after=[tok["cnt", 0]] if h else [], chain=False, sig="cnt" + n)
                if h:
                    tok["acc"] = act(T.sgn[:], T.cnt[:], F.Sign, bias=128.5, scale=-1.0, acc=T.acc[:, 0:1],
                                     after=[tok["cnt", 0], tok["cnt", 1]], chain=False, sig="acc")
            elif s == 14:
                ts(T.d0[:, a:b], T.st[:, a:b], 0.0, A.is_equal, -4096.0 * EPS, A.add, lane=h)
            elif s == 15:
                scan(T.hh[:, a:b], T.d0[:, a:b], T.val[:, a:b], init(T.hh, a - 1, 0.0), A.add, A.min,
                     after=[tok["val", h]], lane=h)
            elif s == 16:
                scan(T.he[:, a:b], T.m16[:, a:b], T.hh[:, a:b], 0.0, A.add, A.min, after=[cm16], lane=h)
            elif s == 17:
                ts(T.hi[:, ka:kb], T.he[:, a + 15:b:16], 4095.0 / 4096.0 / EPS, A.mult, T.hcol[:, 0:1], A.add, lane=h)
                if not h:
                    tok["hu"] = ts(T.hu[:, 0:K], T.pw2[:, 0:K], T.acc[:, 0:1], A.is_lt, float(C), A.mult,
                                   after=[tok["acc"]], chain=False, sig="hu")
            elif s == 18:
                ts(T.hj[:, ka:kb], T.hi[:, ka:kb], 4095, A.bitwise_and, lane=h)
                if not h:
                    tok["h1"] = tt(T.h1[:, 0:K], T.hu[:, 0:K], T.pw[:, 0:K], A.add, after=[tok["hu"]], chain=False, sig="h1")
            elif s == 19:
                tt(T.hf[:, ka:kb], T.hj[:, ka:kb], T.h1[:, ka:kb], A.max, after=[tok["h1"]], lane=h)
            elif s == 20:
                tok["off", h] = cp(T.off[:, ka:kb], T.hf[:, ka:kb], sig="off" + n, lane=h)
            else:
                pre = [tok["off", h], tok["dcp"], plane]
                for j in (0, 1):
                    tok["gv"] = ts(T.gt[:, 4 * a + j:4 * b:4], pl[:, PL * j:PL * j + PL].indirect(T.off[:, ka:kb]),
                                   0.015625, A.mult, after=pre, chain=False, sig="gv")
                for j in (2, 3):
                    tok["gs"] = act(T.gt[:, 4 * a + j:4 * b:4], pl[:, PL * j:PL * j + PL].indirect(T.off[:, ka:kb]),
                                    F.Identity, scale=0.015625, after=pre, chain=False, sig="gs")

        step(0, 0)
        for s in range(21):
            step(s + 1, 0)
            step(s, 1)
        step(21, 1)
        gv, gs = tok["gv"], tok["gs"]
        if t == 2:
            ts(T.hu[:, 0:K], T.hf[:, 0:K], 2.0 * C - 0.5, A.is_gt, -2.0 * C, A.mult, chain=False)
        qg = quant(T.qg[:], T.sg[:], T.gt[:], after=[gv, gs], chain=False, sig="qg")
        gb = ts(T.g64[:, 0:C], T.gt[:, 0:4 * C:4], 64.0, A.mult, chain=False, sig="gb0")
        if t == 2:
            tt(T.ho[:, 0:K], T.hu[:, 0:K], T.hf[:, 0:K], A.add)
        ys = []
        for b in range(4):
            at = PL * b + 2 * C
            r = mm(T.psr[:, 512 * b:512 * b + C], T.qw[:, 128 * b:128 * b + 128], T.sw[:, 128 * b:128 * b + 128],
                   T.qg[:], T.sg[:], after=[qg, ldw], sig="r%d" % b)
            if b:
                gb = act(T.g64[:, C * b:C * b + C], T.gt[:, b:4 * C:4], F.Identity, scale=64.0, after=[gv, gs],
                         chain=False, sig="gb%d" % b)
            ys.append(tt(pn[:, at:at + C], T.psr[:, 512 * b:512 * b + C], T.g64[:, C * b:C * b + C], A.add,
                         after=[gb, r], chain=False, sig="ya%d" % b))
            if t == 2 and b == 0:
                ht = op("V", lambda: V.transpose(T.ht[:], T.ho[:]), sig="ht")
                for n in range(8):
                    dma("Y", T.ot[n, :], T.ht[32 * (n // 2):32 * (n // 2) + K, 16 * (n % 2):16 * (n % 2) + 16],
                        "sto", after=[ht])
        for b in range(3):
            at = PL * b + 2 * C
            xs = act(T.xt[:, b:4 * C:4], pn[:, at:at + C], F.Identity, scale=0.015625, after=[ys[b]],
                     chain=False, sig="xs")
        ts(T.xt[:, 3:4 * C:4], pn[:, PL * 3 + 2 * C:PL * 4], 0.015625, A.mult, after=[ys[3]], chain=False)
        qx = quant(T["qx%d" % (t + 1)][:], T["sx%d" % (t + 1)][:], T.xt[:], after=[xs], sig="qx")

    ym = mm(T.psa[:, 0:C], T.qv[:], T.sv[:], T.qx3[:], T.sx3[:], after=[qx, qv], sig="ym")
    dma("Y", T.oc[:], u8(T.qx3[:]), "stc", after=[qx])
    for k in range(4):
        dma("Y", T.osc[4 * k:4 * k + 4, :], T.sx3[32 * k:32 * k + 4, :], "stc", after=[qx])
    yc = cp(T.yb[:], T.psa[:, 0:C], after=[ym], chain=False, sig="yc")
    dma("S", T.y[:], T.yb[:], "sty", after=[yc])
    for name in cnt:
        if max(seen[e].get(name, 0) for e in seen) < cnt[name]:
            wait("G", (name, cnt[name]))
